import numpy as np
import ml_dtypes


def mxq(x, axis, fmt="e4m3"):
    dtype, down = {"e4m3": (ml_dtypes.float8_e4m3fn, 7), "e5m2": (ml_dtypes.float8_e5m2, 14)}[fmt]
    v = np.moveaxis(np.asarray(x, np.float32).astype(ml_dtypes.bfloat16).astype(np.float64), axis, -1)
    blocks = v.reshape(v.shape[:-1] + (-1, 32))
    amax = np.abs(blocks).max(-1, keepdims=True)
    byte = np.maximum(np.where(amax > 0, np.frexp(amax)[1] - 1 + 127, 0) - down, 1)
    scale = np.exp2(byte - 127.0)
    codes = (blocks / scale).astype(np.float32).astype(dtype).astype(np.float64)
    return np.moveaxis((codes * scale).reshape(v.shape), -1, axis)


WIDE = False


def mx_kscale(k):
    if not WIDE:
        return np.ones(k)
    levels = np.array([10, -10, 5, -5, 0])
    if k % 512:
        return np.exp2(np.random.permutation(np.resize(levels, k // 32))).repeat(32)
    a = np.empty((k // 512, 16))
    for p in range(k // 512):
        a[p, :8] = np.random.permutation(np.resize(levels, 8))
        for g in range(8):
            far = levels[np.abs(levels - a[p, g]) >= 10]
            a[p, g + 8] = far[np.random.randint(len(far))]
    return np.exp2(a.ravel()).repeat(32)


def f64(x):
    return np.asarray(x).astype(np.float64)


def striped(idx):
    return np.tile(idx.reshape(-1, 16).T, (8, 1)).astype(np.uint16)


def unstriped(offs):
    return offs[:16].T.reshape(-1).astype(np.int64)


E2M1 = np.array([0.0, 0.5, 1.0, 1.5, 2.0, 3.0, 4.0, 6.0, -0.0, -0.5, -1.0, -1.5, -2.0, -3.0, -4.0, -6.0])


def pack_weight(w, fmt):
    k, n = w.shape
    w = f64(np.asarray(w, np.float32).astype(ml_dtypes.bfloat16)).reshape(k // 32, 32, n)
    amax = np.abs(w).max(1)
    if fmt == "e4m3":
        byte = np.frexp(amax)[1] - 1 + 127 - 7
    else:
        mant, ex = np.frexp(amax / 6.0)
        byte = np.where(mant > 0.5, ex, ex - 1) + 127
    byte = np.clip(np.where(amax > 0, byte, 1), 1, 254)
    scaled = (w * np.exp2(127.0 - byte)[:, None, :]).reshape(k, n).astype(np.float32)
    by_word = np.ascontiguousarray(scaled.reshape(k // 512, 128, 4, n).transpose(0, 1, 3, 2))
    if fmt == "e4m3":
        words = by_word.astype(ml_dtypes.float8_e4m3fn).view(np.uint8)
    else:
        c = by_word.astype(ml_dtypes.float4_e2m1fn).view(np.uint8) & 0xF
        words = (c[..., 0::2] | (c[..., 1::2] << 4)).reshape(k // 512, 128, 2 * n)
    return np.ascontiguousarray(words), np.ascontiguousarray(byte.astype(np.uint8).reshape(k // 512, 16, n))


def unpack_weight(words, scales, fmt):
    g, _, n = scales.shape
    words = np.ascontiguousarray(words).reshape(g, 128, n, -1)
    if fmt == "e4m3":
        vals = words.view(ml_dtypes.float8_e4m3fn).astype(np.float64)
    else:
        nib = np.empty((g, 128, n, 4), np.uint8)
        nib[..., 0::2] = words & 0xF
        nib[..., 1::2] = words >> 4
        vals = E2M1[nib]
    vals = vals * np.repeat(np.exp2(scales.astype(np.float64) - 127.0), 8, axis=1)[..., None]
    return vals.transpose(0, 1, 3, 2).reshape(g * 512, n)


def gelu(v):
    return 0.5 * v * (1.0 + np.tanh(np.sqrt(2.0 / np.pi) * (v + 0.044715 * v**3)))


K, T, E, C, H, HS, N = 512, 768, 6, 128, 512, 512, 256


def by_expert(wq, xq):
    return np.concatenate([wq[e].T @ xq[:, e * C:(e + 1) * C] for e in range(E)], axis=1)


def setup_inputs():
    n = np.random.standard_normal
    s = mx_kscale(K)
    u = mx_kscale(H)
    v = mx_kscale(HS)
    slot_token = np.random.permutation(T)[:E * C]
    x = pack_weight(n((K, T)) * s[:, None], "e4m3")
    w1 = [pack_weight(m, "e2m1") for m in n((E, K, H)) / np.sqrt(K) / s[None, :, None] * u]
    w2 = [pack_weight(m, "e2m1") for m in n((E, H, N)) / np.sqrt(H) / u[None, :, None]]
    w1s = pack_weight(n((K, HS)) / np.sqrt(K) / s[:, None] * v, "e4m3")
    w2s = pack_weight(n((HS, N)) / np.sqrt(HS) / v[:, None], "e4m3")
    return {
        "x_words": x[0],
        "x_scales": x[1],
        "w1_words": np.stack([m[0] for m in w1]),
        "w1_scales": np.stack([m[1] for m in w1]),
        "w2_words": np.stack([m[0] for m in w2]),
        "w2_scales": np.stack([m[1] for m in w2]),
        "w1s_words": w1s[0],
        "w1s_scales": w1s[1],
        "w2s_words": w2s[0],
        "w2s_scales": w2s[1],
        "gate": np.tile(np.random.uniform(0.2, 1.0, E * C), (128, 1)).astype(np.float32),
        "offs": striped(slot_token),
    }


def reference(x_words, x_scales, w1_words, w1_scales, w2_words, w2_scales, w1s_words, w1s_scales, w2s_words, w2s_scales, gate, offs):
    w1 = np.stack([unpack_weight(w1_words[e], w1_scales[e], "e2m1") for e in range(E)])
    w2 = np.stack([unpack_weight(w2_words[e], w2_scales[e], "e2m1") for e in range(E)])
    w1s = unpack_weight(w1s_words, w1s_scales, "e4m3")
    w2s = unpack_weight(w2s_words, w2s_scales, "e4m3")
    idx = unstriped(offs)
    x = unpack_weight(x_words, x_scales, "e4m3")
    hs = gelu(w1s.T @ x)
    ys = w2s.T @ mxq(hs, 0, "e4m3")
    h = gelu(by_expert(w1, x[:, idx]))
    y = by_expert(w2, mxq(h, 0, "e4m3"))
    c = np.zeros((N, T))
    c[:, idx] = f64(gate[:1]) * y
    return ys + c

@@ -1,0 +1,210 @@
+from contextlib import ExitStack
+
+import concourse.mybir as mybir
+from concourse.masks import make_identity
+
+K, T, E, C, H, HS, N = 512, 768, 6, 128, 512, 512, 256
+FLOPS = 2 * T * (K * H + H * N + K * HS + HS * N)
+
+F32 = mybir.dt.float32
+BF16 = mybir.dt.bfloat16
+I32 = mybir.dt.int32
+U32 = mybir.dt.uint32
+U16 = mybir.dt.uint16
+U8 = mybir.dt.uint8
+FP8X4 = mybir.dt.float8_e4m3fn_x4
+FP4X4 = mybir.dt.float4_e2m1fn_x4
+GELU = mybir.ActivationFunctionType.Gelu_apprx_tanh
+MULT = mybir.AluOpType.mult
+ADD = mybir.AluOpType.add
+
+P = 128
+PACK = 4
+NB = N // P
+CHUNK = 256
+GATHER_GROUPS = ((0, 1), (1, 3), (3, 6))
+
+
+def tile_moe_shf_mlp_gelu_kernel(
+    tc, x_words, x_scales, w1_words, w1_scales, w2_words, w2_scales,
+    w1s_words, w1s_scales, w2s_words, w2s_scales, gate, offs, out,
+):
+    nc = tc.nc
+    with ExitStack() as ctx:
+        keep = ctx.enter_context(tc.tile_pool(name="keep", bufs=1))
+        ring = ctx.enter_context(tc.tile_pool(name="ring", bufs=3))
+        ps_l1 = ctx.enter_context(tc.psum_pool(name="ps_l1", bufs=3))
+        ps_one = ctx.enter_context(tc.psum_pool(name="ps_one", bufs=1))
+
+        offsets = keep.tile([P, T // 16], U16, name="offsets")
+        xw = keep.tile([P, T], U32, name="xw", align_bytes=64)
+        xs = keep.tile([P, T], U8, name="xs", align_bytes=64)
+        w1w = [keep.tile([P, b - a, 2 * H], U8, name="w1w%d" % a, align_bytes=64) for a, b in GATHER_GROUPS]
+        w1sc = keep.tile([P, E, H], U8, name="w1sc", align_bytes=64)
+        w2w = keep.tile([P, E, 2 * N], U8, name="w2w", align_bytes=64)
+        w2sc = keep.tile([P, E, N], U8, name="w2sc", align_bytes=64)
+        v1w = keep.tile([P, HS], I32, name="v1w", align_bytes=64)
+        v1sc = keep.tile([P, HS], U8, name="v1sc", align_bytes=64)
+        v1w_perm = keep.tile([P, HS], I32, name="v1w_perm", align_bytes=64)
+        v1sc_perm = keep.tile([P, HS], U8, name="v1sc_perm", align_bytes=64)
+        v2w = keep.tile([P, N], I32, name="v2w", align_bytes=64)
+        v2sc = keep.tile([P, N], U8, name="v2sc", align_bytes=64)
+        g = keep.tile([P, T], F32, name="g")
+        ident = keep.tile([P, P], F32, name="ident")
+        y_sb = keep.tile([P, NB, T], F32, name="y_sb")
+        win = [keep.tile([P, T], F32, name="win%d" % nb) for nb in range(NB)]
+
+        def load_plane(queue, plane, scales):
+            rows = scales[0].bitcast(I32).rearrange("(q r) c -> r q c", r=4)
+            for r in range(4):
+                queue.dma_start(out=plane[:].bitcast(I32)[r:P:32], in_=rows[r])
+
+        def load_expert_planes(queue, plane, scales):
+            rows = scales[:, 0].bitcast(I32).rearrange("e (q r) c -> r q e c", r=4)
+            for r in range(4):
+                queue.dma_start(out=plane[:].bitcast(I32)[r:P:32], in_=rows[r])
+
+        def load_w1(queue, i):
+            a, b = GATHER_GROUPS[i]
+            queue.dma_start(out=w1w[i][:].bitcast(I32), in_=w1_words[a:b, 0].bitcast(I32).rearrange("e p c -> p e c"))
+
+        for plane in (xs, w1sc, w2sc, v1sc, v2sc):
+            nc.vector.memset(plane[:].bitcast(I32), 0)
+        make_identity(nc, ident[:])
+
+        nc.sync.dma_start(offsets[:], offs)
+        nc.scalar.dma_start(out=xw[:].bitcast(I32), in_=x_words[0].rearrange("p t d -> p (t d)").bitcast(I32))
+        load_plane(nc.sync, xs, x_scales)
+        load_expert_planes(nc.sync, w1sc, w1_scales)
+        load_w1(nc.sync, 0)
+        load_w1(nc.sync, 1)
+        load_expert_planes(nc.sync, w2sc, w2_scales)
+        nc.sync.dma_start(out=w2w[:].bitcast(I32), in_=w2_words[:, 0].bitcast(I32).rearrange("e p c -> p e c"))
+        nc.sync.dma_start(out=g[:], in_=gate)
+        load_w1(nc.sync, 2)
+        nc.sync.dma_start(out=v1w[:], in_=w1s_words[0].rearrange("p l d -> p (l d)").bitcast(I32))
+        load_plane(nc.sync, v1sc, w1s_scales)
+        nc.sync.dma_start(out=v2w[:], in_=w2s_words[0].rearrange("p n d -> p (n d)").bitcast(I32))
+        load_plane(nc.sync, v2sc, w2s_scales)
+
+        slot_words, slot_scales, w1_of = {}, {}, {}
+
+        def gather(i):
+            a, b = GATHER_GROUPS[i]
+            words = keep.tile([P, (b - a) * C], U32, name="xgw%d" % i, align_bytes=64)
+            scales = keep.tile([P, (b - a) * C], U8, name="xgs%d" % i, align_bytes=64)
+            piece = offsets[:, a * C // 16 : b * C // 16]
+            nc.vector.tensor_copy(out=words[:], in_=xw[:].indirect(piece))
+            nc.vector.tensor_copy(out=scales[:], in_=xs[:].indirect(piece))
+            for e in range(a, b):
+                slot_words[e] = words[:, (e - a) * C : (e - a + 1) * C]
+                slot_scales[e] = scales[:, (e - a) * C : (e - a + 1) * C]
+                w1_of[e] = w1w[i][:, e - a, :]
+
+        h_codes = {}
+
+        def routed_first(e):
+            pre = ps_l1.tile([P, H], F32, name="pre", tag="l1")
+            nc.tensor.matmul_mx(
+                out=pre[:], lhsT=slot_words[e].bitcast(FP8X4), lhsT_scale=slot_scales[e],
+                rhs=w1_of[e].bitcast(FP4X4), rhs_scale=w1sc[:, e, :], start=True, stop=True,
+            )
+            h_rows = ring.tile([P, H], BF16, name="h_rows", align_bytes=64)
+            nc.scalar.activation(
+                out=h_rows[:].rearrange("s (u p v) -> s u p v", u=2, v=2),
+                in_=pre[:].rearrange("s (p u v) -> s u p v", u=2, v=2), func=GELU,
+            )
+            turned = ps_one.tile([P, 2, C], F32, name="turned")
+            pairs = h_rows[:].bitcast(F32)
+            for u in range(2):
+                nc.tensor.transpose(turned[:, u, :], pairs[:, u * P : (u + 1) * P], ident[:])
+            h_in = ring.tile([P, C * PACK], BF16, name="h_in", align_bytes=64)
+            nc.scalar.copy(
+                out=h_in[:].bitcast(F32).rearrange("p (s u) -> p s u", u=2),
+                in_=turned[:].rearrange("p u s -> p s u"),
+            )
+            codes = ring.tile([P, C], U32, name="h_codes", align_bytes=64)
+            scales = ring.tile([P, C], U8, name="h_scales", align_bytes=64)
+            nc.vector.quantize_mx(out=codes[:].bitcast(FP8X4), scales=scales[:], in_=h_in[:])
+            h_codes[e] = (codes, scales)
+
+        def routed_second(e):
+            codes, scales = h_codes[e]
+            y = ps_one.tile([P, NB, C], F32, name="y")
+            for nb in range(NB):
+                nc.tensor.matmul_mx(
+                    out=y[:, nb, :], lhsT=w2w[:, e, 2 * nb * P : 2 * (nb + 1) * P].bitcast(FP4X4),
+                    lhsT_scale=w2sc[:, e, nb * P : (nb + 1) * P],
+                    rhs=codes[:].bitcast(FP8X4), rhs_scale=scales[:], start=True, stop=True,
+                )
+            nc.scalar.copy(out=y_sb[:, :, e * C : (e + 1) * C], in_=y[:])
+
+        def scatter(a, b, nb):
+            nc.vector.tensor_tensor(
+                out=win[nb][:].indirect(offsets[:, a * C // 16 : b * C // 16]),
+                in0=y_sb[:, nb, a * C : b * C], in1=g[:, a * C : b * C], op=MULT,
+            )
+
+        hs_in = [keep.tile([P, CHUNK * PACK], BF16, name="hs_in%d" % c, align_bytes=64) for c in range(T // CHUNK)]
+        ys = {}
+
+        def shared_first(tb):
+            pre = ps_l1.tile([P, PACK, P], F32, name="pre_s", tag="l1")
+            cols = slice(tb * P, (tb + 1) * P)
+            for d in range(PACK):
+                nc.tensor.matmul_mx(
+                    out=pre[:, d, :], lhsT=v1w_perm[:, d * P : (d + 1) * P].bitcast(FP8X4),
+                    lhsT_scale=v1sc_perm[:, d * P : (d + 1) * P],
+                    rhs=xw[:, cols].bitcast(FP8X4), rhs_scale=xs[:, cols], start=True, stop=True,
+                )
+            c, half = divmod(tb, 2)
+            nc.scalar.activation(
+                out=hs_in[c][:, half * P * PACK : (half + 1) * P * PACK].rearrange("p (t d) -> p t d", d=PACK),
+                in_=pre[:].rearrange("p d t -> p t d"), func=GELU,
+            )
+
+        def shared_second(c):
+            codes = keep.tile([P, CHUNK], U32, name="hs_codes%d" % c, align_bytes=64)
+            scales = keep.tile([P, CHUNK], U8, name="hs_scales%d" % c, align_bytes=64)
+            nc.vector.quantize_mx(out=codes[:].bitcast(FP8X4), scales=scales[:], in_=hs_in[c][:])
+            ys[c] = ps_one.tile([P, NB, CHUNK], F32, name="ys%d" % c)
+            for nb in range(NB):
+                nc.tensor.matmul_mx(
+                    out=ys[c][:, nb, :], lhsT=v2w[:, nb * P : (nb + 1) * P].bitcast(FP8X4),
+                    lhsT_scale=v2sc[:, nb * P : (nb + 1) * P],
+                    rhs=codes[:].bitcast(FP8X4), rhs_scale=scales[:], start=True, stop=True,
+                )
+
+        def finish(nb):
+            for c in range(T // CHUNK):
+                cols = slice(c * CHUNK, (c + 1) * CHUNK)
+                res = keep.tile([P, CHUNK], F32, name="res%d_%d" % (nb, c))
+                nc.vector.tensor_tensor(out=res[:], in0=ys[c][:, nb, :], in1=win[nb][:, cols], op=ADD)
+                nc.sync.dma_start(out=out[nb * P : (nb + 1) * P, cols], in_=res[:])
+
+        gather(0)
+        gather(1)
+        gather(2)
+        nc.vector.tensor_copy(
+            out=v1w_perm[:].rearrange("p (d m) -> p d m", d=PACK), in_=v1w[:].rearrange("p (m d) -> p d m", d=PACK)
+        )
+        nc.vector.tensor_copy(
+            out=v1sc_perm[:].rearrange("p (d m) -> p d m", d=PACK), in_=v1sc[:].rearrange("p (m d) -> p d m", d=PACK)
+        )
+        routed_first(0)
+        for e in range(1, E):
+            routed_first(e)
+            shared_first(e - 1)
+            if e == E - 1:
+                shared_first(e)
+            if e % 2 == 0:
+                shared_second(e // 2 - 1)
+            if e == E - 1:
+                shared_second(T // CHUNK - 1)
+            routed_second(e - 1)
+            for nb in range(NB):
+                scatter(e - 1, e, nb)
+        routed_second(E - 1)
+        for nb in range(NB):
+            scatter(E - 1, E, nb)
+            finish(nb)

@@ -22,6 +22,11 @@ P = 128
 PACK = 4
 NB = N // P
 CHUNK = 256
+ROUTED_PRE = (0, 1, 0, 7, 7, 7)
+ROUTED_TURN = (2, 6, 2, 3, 2, 3)
+ROUTED_Y = (7, 2, 3, 2, 3, 2)
+SHARED_PRE = (1, 4, 1, 4, 1, 4)
+SHARED_Y = (3, 2, 5)
 GATHER_GROUPS = ((0, 1), (1, 3), (3, 6))
 
 
@@ -32,9 +37,10 @@ def tile_moe_shf_mlp_gelu_kernel(
     nc = tc.nc
     with ExitStack() as ctx:
         keep = ctx.enter_context(tc.tile_pool(name="keep", bufs=1))
-        ring = ctx.enter_context(tc.tile_pool(name="ring", bufs=3))
-        ps_l1 = ctx.enter_context(tc.psum_pool(name="ps_l1", bufs=3))
-        ps_one = ctx.enter_context(tc.psum_pool(name="ps_one", bufs=1))
+        ring = ctx.enter_context(tc.tile_pool(name="ring", bufs=4))
+        slots = ctx.enter_context(tc.tile_pool(name="slots", bufs=2))
+        psum = ctx.enter_context(tc.psum_pool(name="psum", bufs=1))
+        bank = [psum.tile([P, 512], F32, name="bank%d" % i) for i in range(8)]
 
         offsets = keep.tile([P, T // 16], U16, name="offsets")
         xw = keep.tile([P, T], U32, name="xw", align_bytes=64)
@@ -45,19 +51,19 @@ def tile_moe_shf_mlp_gelu_kernel(
         w2sc = keep.tile([P, E, N], U8, name="w2sc", align_bytes=64)
         v1w = keep.tile([P, HS], I32, name="v1w", align_bytes=64)
         v1sc = keep.tile([P, HS], U8, name="v1sc", align_bytes=64)
-        v1w_perm = keep.tile([P, HS], I32, name="v1w_perm", align_bytes=64)
-        v1sc_perm = keep.tile([P, HS], U8, name="v1sc_perm", align_bytes=64)
         v2w = keep.tile([P, N], I32, name="v2w", align_bytes=64)
         v2sc = keep.tile([P, N], U8, name="v2sc", align_bytes=64)
         g = keep.tile([P, T], F32, name="g")
         ident = keep.tile([P, P], F32, name="ident")
-        y_sb = keep.tile([P, NB, T], F32, name="y_sb")
         win = [keep.tile([P, T], F32, name="win%d" % nb) for nb in range(NB)]
 
-        def load_plane(queue, plane, scales):
-            rows = scales[0].bitcast(I32).rearrange("(q r) c -> r q c", r=4)
-            for r in range(4):
-                queue.dma_start(out=plane[:].bitcast(I32)[r:P:32], in_=rows[r])
+        def load_full_plane(queue, plane, scales):
+            rows = scales[0].bitcast(I32).rearrange("(q r) c -> q r c", r=4)
+            for q in range(4):
+                queue.dma_start(
+                    out=plane[:].bitcast(I32)[32 * q : 32 * (q + 1)],
+                    in_=rows[q].unsqueeze(0).to_broadcast([8, 4, rows.shape[2]]),
+                )
 
         def load_expert_planes(queue, plane, scales):
             rows = scales[:, 0].bitcast(I32).rearrange("e (q r) c -> r q e c", r=4)
@@ -68,31 +74,32 @@ def tile_moe_shf_mlp_gelu_kernel(
             a, b = GATHER_GROUPS[i]
             queue.dma_start(out=w1w[i][:].bitcast(I32), in_=w1_words[a:b, 0].bitcast(I32).rearrange("e p c -> p e c"))
 
-        for plane in (xs, w1sc, w2sc, v1sc, v2sc):
-            nc.vector.memset(plane[:].bitcast(I32), 0)
+        for plane in (w1sc, w2sc):
+            nc.gpsimd.memset(plane[:, : E // 2, :].bitcast(I32), 0)
+            nc.vector.memset(plane[:, E // 2 :, :].bitcast(I32), 0)
         make_identity(nc, ident[:])
 
         nc.sync.dma_start(offsets[:], offs)
-        nc.scalar.dma_start(out=xw[:].bitcast(I32), in_=x_words[0].rearrange("p t d -> p (t d)").bitcast(I32))
-        load_plane(nc.sync, xs, x_scales)
-        load_expert_planes(nc.sync, w1sc, w1_scales)
+        load_full_plane(nc.sync, xs, x_scales)
+        nc.sync.dma_start(out=xw[:].bitcast(I32), in_=x_words[0].rearrange("p t d -> p (t d)").bitcast(I32))
         load_w1(nc.sync, 0)
+        load_expert_planes(nc.sync, w1sc, w1_scales)
         load_w1(nc.sync, 1)
-        load_expert_planes(nc.sync, w2sc, w2_scales)
-        nc.sync.dma_start(out=w2w[:].bitcast(I32), in_=w2_words[:, 0].bitcast(I32).rearrange("e p c -> p e c"))
-        nc.sync.dma_start(out=g[:], in_=gate)
-        load_w1(nc.sync, 2)
         nc.sync.dma_start(out=v1w[:], in_=w1s_words[0].rearrange("p l d -> p (l d)").bitcast(I32))
-        load_plane(nc.sync, v1sc, w1s_scales)
+        load_full_plane(nc.sync, v1sc, w1s_scales)
+        nc.sync.dma_start(out=w2w[:].bitcast(I32), in_=w2_words[:, 0].bitcast(I32).rearrange("e p c -> p e c"))
+        load_expert_planes(nc.sync, w2sc, w2_scales)
+        load_w1(nc.sync, 2)
+        nc.sync.dma_start(out=g[:], in_=gate)
         nc.sync.dma_start(out=v2w[:], in_=w2s_words[0].rearrange("p n d -> p (n d)").bitcast(I32))
-        load_plane(nc.sync, v2sc, w2s_scales)
+        load_full_plane(nc.sync, v2sc, w2s_scales)
 
         slot_words, slot_scales, w1_of = {}, {}, {}
 
         def gather(i):
             a, b = GATHER_GROUPS[i]
-            words = keep.tile([P, (b - a) * C], U32, name="xgw%d" % i, align_bytes=64)
-            scales = keep.tile([P, (b - a) * C], U8, name="xgs%d" % i, align_bytes=64)
+            words = keep.tile([P, (b - a) * C], U32, name="xgw", tag="xgw%d" % i, align_bytes=64)
+            scales = slots.tile([P, (b - a) * C], U8, name="xgs", tag="plane", align_bytes=64)
             piece = offsets[:, a * C // 16 : b * C // 16]
             nc.vector.tensor_copy(out=words[:], in_=xw[:].indirect(piece))
             nc.vector.tensor_copy(out=scales[:], in_=xs[:].indirect(piece))
@@ -103,25 +110,34 @@ def tile_moe_shf_mlp_gelu_kernel(
 
         h_codes = {}
 
-        def routed_first(e):
-            pre = ps_l1.tile([P, H], F32, name="pre", tag="l1")
+        def activate(pre, words, scales, w, w_scales, turned):
             nc.tensor.matmul_mx(
-                out=pre[:], lhsT=slot_words[e].bitcast(FP8X4), lhsT_scale=slot_scales[e],
-                rhs=w1_of[e].bitcast(FP4X4), rhs_scale=w1sc[:, e, :], start=True, stop=True,
+                out=pre[:], lhsT=words.bitcast(FP8X4), lhsT_scale=scales, rhs=w, rhs_scale=w_scales,
+                start=True, stop=True,
             )
             h_rows = ring.tile([P, H], BF16, name="h_rows", align_bytes=64)
             nc.scalar.activation(
                 out=h_rows[:].rearrange("s (u p v) -> s u p v", u=2, v=2),
                 in_=pre[:].rearrange("s (p u v) -> s u p v", u=2, v=2), func=GELU,
             )
-            turned = ps_one.tile([P, 2, C], F32, name="turned")
             pairs = h_rows[:].bitcast(F32)
             for u in range(2):
                 nc.tensor.transpose(turned[:, u, :], pairs[:, u * P : (u + 1) * P], ident[:])
+
+        routed_turned = {}
+
+        def routed_activate(e):
+            routed_turned[e] = bank[ROUTED_TURN[e]][:, : 2 * C].rearrange("p (u s) -> p u s", u=2)
+            activate(
+                bank[ROUTED_PRE[e]], slot_words[e], slot_scales[e], w1_of[e].bitcast(FP4X4), w1sc[:, e, :],
+                routed_turned[e],
+            )
+
+        def routed_quantize(e):
             h_in = ring.tile([P, C * PACK], BF16, name="h_in", align_bytes=64)
             nc.scalar.copy(
                 out=h_in[:].bitcast(F32).rearrange("p (s u) -> p s u", u=2),
-                in_=turned[:].rearrange("p u s -> p s u"),
+                in_=routed_turned[e].rearrange("p u s -> p s u"),
             )
             codes = ring.tile([P, C], U32, name="h_codes", align_bytes=64)
             scales = ring.tile([P, C], U8, name="h_scales", align_bytes=64)
@@ -130,26 +146,35 @@ def tile_moe_shf_mlp_gelu_kernel(
 
         def routed_second(e):
             codes, scales = h_codes[e]
-            y = ps_one.tile([P, NB, C], F32, name="y")
+            y = bank[ROUTED_Y[e]][:, : NB * C].rearrange("p (b s) -> p b s", b=NB)
             for nb in range(NB):
                 nc.tensor.matmul_mx(
                     out=y[:, nb, :], lhsT=w2w[:, e, 2 * nb * P : 2 * (nb + 1) * P].bitcast(FP4X4),
                     lhsT_scale=w2sc[:, e, nb * P : (nb + 1) * P],
                     rhs=codes[:].bitcast(FP8X4), rhs_scale=scales[:], start=True, stop=True,
                 )
-            nc.scalar.copy(out=y_sb[:, :, e * C : (e + 1) * C], in_=y[:])
+            y_sb = keep.tile([P, NB, C], F32, name="y_sb%d" % e)
+            nc.scalar.copy(out=y_sb[:], in_=y)
+            for nb in range(NB):
+                nc.vector.tensor_tensor(
+                    out=win[nb][:].indirect(offsets[:, e * C // 16 : (e + 1) * C // 16]),
+                    in0=y_sb[:, nb, :], in1=g[:, e * C : (e + 1) * C], op=MULT,
+                )
 
-        def scatter(a, b, nb):
-            nc.vector.tensor_tensor(
-                out=win[nb][:].indirect(offsets[:, a * C // 16 : b * C // 16]),
-                in0=y_sb[:, nb, a * C : b * C], in1=g[:, a * C : b * C], op=MULT,
-            )
-
-        hs_in = [keep.tile([P, CHUNK * PACK], BF16, name="hs_in%d" % c, align_bytes=64) for c in range(T // CHUNK)]
         ys = {}
+        hs_in = [keep.tile([P, CHUNK * PACK], BF16, name="hs_in%d" % c, align_bytes=64) for c in range(T // CHUNK)]
 
-        def shared_first(tb):
-            pre = ps_l1.tile([P, PACK, P], F32, name="pre_s", tag="l1")
+        def permute_shared():
+            words = keep.tile([P, HS], I32, name="v1w_perm", tag="xgw0", align_bytes=64)
+            scales = slots.tile([P, HS], U8, name="v1sc_perm", tag="plane", align_bytes=64)
+            for dest, src in ((words, v1w), (scales, v1sc)):
+                nc.vector.tensor_copy(
+                    out=dest[:].rearrange("p (d m) -> p d m", d=PACK), in_=src[:].rearrange("p (m d) -> p d m", d=PACK)
+                )
+            return words, scales
+
+        def shared_activate(tb):
+            pre = bank[SHARED_PRE[tb]][:].rearrange("p (d t) -> p d t", d=PACK)
             cols = slice(tb * P, (tb + 1) * P)
             for d in range(PACK):
                 nc.tensor.matmul_mx(
@@ -160,14 +185,14 @@ def tile_moe_shf_mlp_gelu_kernel(
             c, half = divmod(tb, 2)
             nc.scalar.activation(
                 out=hs_in[c][:, half * P * PACK : (half + 1) * P * PACK].rearrange("p (t d) -> p t d", d=PACK),
-                in_=pre[:].rearrange("p d t -> p t d"), func=GELU,
+                in_=pre.rearrange("p d t -> p t d"), func=GELU,
             )
 
         def shared_second(c):
             codes = keep.tile([P, CHUNK], U32, name="hs_codes%d" % c, align_bytes=64)
             scales = keep.tile([P, CHUNK], U8, name="hs_scales%d" % c, align_bytes=64)
             nc.vector.quantize_mx(out=codes[:].bitcast(FP8X4), scales=scales[:], in_=hs_in[c][:])
-            ys[c] = ps_one.tile([P, NB, CHUNK], F32, name="ys%d" % c)
+            ys[c] = bank[SHARED_Y[c]][:].rearrange("p (b t) -> p b t", b=NB)
             for nb in range(NB):
                 nc.tensor.matmul_mx(
                     out=ys[c][:, nb, :], lhsT=v2w[:, nb * P : (nb + 1) * P].bitcast(FP8X4),
@@ -175,36 +200,35 @@ def tile_moe_shf_mlp_gelu_kernel(
                     rhs=codes[:].bitcast(FP8X4), rhs_scale=scales[:], start=True, stop=True,
                 )
 
-        def finish(nb):
-            for c in range(T // CHUNK):
-                cols = slice(c * CHUNK, (c + 1) * CHUNK)
-                res = keep.tile([P, CHUNK], F32, name="res%d_%d" % (nb, c))
-                nc.vector.tensor_tensor(out=res[:], in0=ys[c][:, nb, :], in1=win[nb][:, cols], op=ADD)
-                nc.sync.dma_start(out=out[nb * P : (nb + 1) * P, cols], in_=res[:])
+        def finish(c, nb):
+            cols = slice(c * CHUNK, (c + 1) * CHUNK)
+            res = keep.tile([P, CHUNK], F32, name="res%d_%d" % (nb, c))
+            nc.vector.tensor_tensor(out=res[:], in0=ys[c][:, nb, :], in1=win[nb][:, cols], op=ADD)
+            nc.sync.dma_start(out=out[nb * P : (nb + 1) * P, cols], in_=res[:])
 
         gather(0)
         gather(1)
+        routed_activate(0)
+        routed_activate(1)
+        routed_quantize(0)
         gather(2)
-        nc.vector.tensor_copy(
-            out=v1w_perm[:].rearrange("p (d m) -> p d m", d=PACK), in_=v1w[:].rearrange("p (m d) -> p d m", d=PACK)
-        )
-        nc.vector.tensor_copy(
-            out=v1sc_perm[:].rearrange("p (d m) -> p d m", d=PACK), in_=v1sc[:].rearrange("p (m d) -> p d m", d=PACK)
-        )
-        routed_first(0)
+        routed_quantize(1)
+        routed_second(0)
+        routed_activate(2)
+        v1w_perm, v1sc_perm = permute_shared()
+        blocks = list(range(T // P))
         for e in range(1, E):
-            routed_first(e)
-            shared_first(e - 1)
-            if e == E - 1:
-                shared_first(e)
-            if e % 2 == 0:
-                shared_second(e // 2 - 1)
-            if e == E - 1:
-                shared_second(T // CHUNK - 1)
-            routed_second(e - 1)
+            if e + 1 < E:
+                routed_quantize(e + 1)
+            if e + 2 < E:
+                routed_activate(e + 2)
+            else:
+                shared_activate(blocks.pop(0))
+            if e + 1 < E:
+                shared_activate(blocks.pop(0))
+            routed_second(e)
+        for c in range(T // CHUNK):
+            shared_second(c)
+        for c in range(T // CHUNK):
             for nb in range(NB):
-                scatter(e - 1, e, nb)
-        routed_second(E - 1)
-        for nb in range(NB):
-            scatter(E - 1, E, nb)
-            finish(nb)
+                finish(c, nb)

@@ -22,11 +22,11 @@ P = 128
 PACK = 4
 NB = N // P
 CHUNK = 256
-ROUTED_PRE = (0, 1, 0, 7, 7, 7)
-ROUTED_TURN = (2, 6, 2, 3, 2, 3)
-ROUTED_Y = (7, 2, 3, 2, 3, 2)
-SHARED_PRE = (1, 4, 1, 4, 1, 4)
-SHARED_Y = (3, 2, 5)
+ROUTED_PRE = (0, 1, 0, 0, 0, 0)
+ROUTED_TURN = (2, 3, 4, 2, 3, 4)
+ROUTED_Y = (3, 4, 2, 3, 4, 2)
+SHARED_PRE = (3, 4, 2, 3, 0, 0)
+SHARED_Y = (4, 0, 5)
 GATHER_GROUPS = ((0, 1), (1, 3), (3, 6))
 
 
@@ -213,19 +213,17 @@ def tile_moe_shf_mlp_gelu_kernel(
         routed_quantize(0)
         gather(2)
         routed_quantize(1)
-        routed_second(0)
         routed_activate(2)
         v1w_perm, v1sc_perm = permute_shared()
-        blocks = list(range(T // P))
+        routed_second(0)
         for e in range(1, E):
             if e + 1 < E:
                 routed_quantize(e + 1)
             if e + 2 < E:
                 routed_activate(e + 2)
-            else:
-                shared_activate(blocks.pop(0))
-            if e + 1 < E:
-                shared_activate(blocks.pop(0))
+            shared_activate(e - 1)
+            if e == E - 1:
+                shared_activate(e)
             routed_second(e)
         for c in range(T // CHUNK):
             shared_second(c)

@@ -22,10 +22,10 @@ P = 128
 PACK = 4
 NB = N // P
 CHUNK = 256
-ROUTED_PRE = (0, 1, 0, 0, 0, 0)
+ROUTED_PRE = (0, 1, 0, 1, 0, 1)
 ROUTED_TURN = (2, 3, 4, 2, 3, 4)
-ROUTED_Y = (3, 4, 2, 3, 4, 2)
-SHARED_PRE = (3, 4, 2, 3, 0, 0)
+ROUTED_Y = (7, 4, 2, 3, 4, 2)
+SHARED_PRE = (1, 0, 2, 3, 1, 0)
 SHARED_Y = (4, 0, 5)
 GATHER_GROUPS = ((0, 1), (1, 3), (3, 6))
 
@@ -110,16 +110,20 @@ def tile_moe_shf_mlp_gelu_kernel(
 
         h_codes = {}
 
-        def activate(pre, words, scales, w, w_scales, turned):
+        def halves(e):
+            return (slice(0, 1), slice(1, 2)) if e == 0 else (slice(0, 2),)
+
+        def activate(pre, words, scales, w, w_scales, turned, parts):
             nc.tensor.matmul_mx(
                 out=pre[:], lhsT=words.bitcast(FP8X4), lhsT_scale=scales, rhs=w, rhs_scale=w_scales,
                 start=True, stop=True,
             )
             h_rows = ring.tile([P, H], BF16, name="h_rows", align_bytes=64)
-            nc.scalar.activation(
-                out=h_rows[:].rearrange("s (u p v) -> s u p v", u=2, v=2),
-                in_=pre[:].rearrange("s (p u v) -> s u p v", u=2, v=2), func=GELU,
-            )
+            for u in parts:
+                nc.scalar.activation(
+                    out=h_rows[:].rearrange("s (u p v) -> s u p v", u=2, v=2)[:, u],
+                    in_=pre[:].rearrange("s (p u v) -> s u p v", u=2, v=2)[:, u], func=GELU,
+                )
             pairs = h_rows[:].bitcast(F32)
             for u in range(2):
                 nc.tensor.transpose(turned[:, u, :], pairs[:, u * P : (u + 1) * P], ident[:])
@@ -130,7 +134,7 @@ def tile_moe_shf_mlp_gelu_kernel(
             routed_turned[e] = bank[ROUTED_TURN[e]][:, : 2 * C].rearrange("p (u s) -> p u s", u=2)
             activate(
                 bank[ROUTED_PRE[e]], slot_words[e], slot_scales[e], w1_of[e].bitcast(FP4X4), w1sc[:, e, :],
-                routed_turned[e],
+                routed_turned[e], halves(e),
             )
 
         def routed_quantize(e):
@@ -154,7 +158,8 @@ def tile_moe_shf_mlp_gelu_kernel(
                     rhs=codes[:].bitcast(FP8X4), rhs_scale=scales[:], start=True, stop=True,
                 )
             y_sb = keep.tile([P, NB, C], F32, name="y_sb%d" % e)
-            nc.scalar.copy(out=y_sb[:], in_=y)
+            for nb in halves(e):
+                nc.scalar.copy(out=y_sb[:, nb], in_=y[:, nb])
             for nb in range(NB):
                 nc.vector.tensor_tensor(
                     out=win[nb][:].indirect(offsets[:, e * C // 16 : (e + 1) * C // 16]),

@@ -21,12 +21,13 @@ ADD = mybir.AluOpType.add
 P = 128
 PACK = 4
 NB = N // P
-CHUNK = 256
-ROUTED_PRE = (0, 1, 0, 1, 0, 1)
-ROUTED_TURN = (2, 3, 4, 2, 3, 4)
-ROUTED_Y = (7, 4, 2, 3, 4, 2)
-SHARED_PRE = (1, 0, 2, 3, 1, 0)
-SHARED_Y = (4, 0, 5)
+CHUNKS = ((0, 256), (256, 768))
+ROUTED_PRE = (0, 1, 0, 1, 0, 7)
+ROUTED_TURN = (2, 3, 7, 4, 2, 3)
+ROUTED_Y = ((7, 7), (4, 4), (7, 4), (2, 2), (5, 5), (4, 4))
+SHARED_PRE = (5, 6, 5, 6, 4, 6)
+W1_GROUPS = ((0, 2), (2, 4), (4, 6))
+W2_GROUPS = ((0, 2), (2, 6))
 GATHER_GROUPS = ((0, 1), (1, 3), (3, 6))
 
 
@@ -37,7 +38,7 @@ def tile_moe_shf_mlp_gelu_kernel(
     nc = tc.nc
     with ExitStack() as ctx:
         keep = ctx.enter_context(tc.tile_pool(name="keep", bufs=1))
-        ring = ctx.enter_context(tc.tile_pool(name="ring", bufs=4))
+        ring = ctx.enter_context(tc.tile_pool(name="ring", bufs=6))
         slots = ctx.enter_context(tc.tile_pool(name="slots", bufs=2))
         psum = ctx.enter_context(tc.psum_pool(name="psum", bufs=1))
         bank = [psum.tile([P, 512], F32, name="bank%d" % i) for i in range(8)]
@@ -45,56 +46,70 @@ def tile_moe_shf_mlp_gelu_kernel(
         offsets = keep.tile([P, T // 16], U16, name="offsets")
         xw = keep.tile([P, T], U32, name="xw", align_bytes=64)
         xs = keep.tile([P, T], U8, name="xs", align_bytes=64)
-        w1w = [keep.tile([P, b - a, 2 * H], U8, name="w1w%d" % a, align_bytes=64) for a, b in GATHER_GROUPS]
+        w1w = [keep.tile([P, b - a, 2 * H], U8, name="w1w%d" % a, align_bytes=64) for a, b in W1_GROUPS]
         w1sc = keep.tile([P, E, H], U8, name="w1sc", align_bytes=64)
-        w2w = keep.tile([P, E, 2 * N], U8, name="w2w", align_bytes=64)
+        w2w = [keep.tile([P, b - a, 2 * N], U8, name="w2w%d" % a, align_bytes=64) for a, b in W2_GROUPS]
         w2sc = keep.tile([P, E, N], U8, name="w2sc", align_bytes=64)
         v1w = keep.tile([P, HS], I32, name="v1w", align_bytes=64)
         v1sc = keep.tile([P, HS], U8, name="v1sc", align_bytes=64)
         v2w = keep.tile([P, N], I32, name="v2w", align_bytes=64)
         v2sc = keep.tile([P, N], U8, name="v2sc", align_bytes=64)
-        g = keep.tile([P, T], F32, name="g")
+        g = [keep.tile([P, (b - a) * C], F32, name="g%d" % a) for a, b in W2_GROUPS]
         ident = keep.tile([P, P], F32, name="ident")
         win = [keep.tile([P, T], F32, name="win%d" % nb) for nb in range(NB)]
 
-        def load_full_plane(queue, plane, scales):
+        def load_plane(queue, plane, scales, r):
+            rows = scales[0].bitcast(I32).rearrange("(q r) c -> r q c", r=4)
+            queue.dma_start(out=plane[:].bitcast(I32)[r:P:32], in_=rows[r])
+
+        def load_full_plane(queue, plane, scales, q):
             rows = scales[0].bitcast(I32).rearrange("(q r) c -> q r c", r=4)
-            for q in range(4):
-                queue.dma_start(
-                    out=plane[:].bitcast(I32)[32 * q : 32 * (q + 1)],
-                    in_=rows[q].unsqueeze(0).to_broadcast([8, 4, rows.shape[2]]),
-                )
+            queue.dma_start(
+                out=plane[:].bitcast(I32)[32 * q : 32 * (q + 1)],
+                in_=rows[q].unsqueeze(0).to_broadcast([8, 4, rows.shape[2]]),
+            )
 
-        def load_expert_planes(queue, plane, scales):
+        def load_expert_planes(queue, plane, scales, r):
             rows = scales[:, 0].bitcast(I32).rearrange("e (q r) c -> r q e c", r=4)
-            for r in range(4):
-                queue.dma_start(out=plane[:].bitcast(I32)[r:P:32], in_=rows[r])
+            queue.dma_start(out=plane[:].bitcast(I32)[r:P:32], in_=rows[r])
 
-        def load_w1(queue, i):
-            a, b = GATHER_GROUPS[i]
-            queue.dma_start(out=w1w[i][:].bitcast(I32), in_=w1_words[a:b, 0].bitcast(I32).rearrange("e p c -> p e c"))
+        def load_words(queue, tile, words, a, b):
+            queue.dma_start(out=tile[:].bitcast(I32), in_=words[a:b, 0].bitcast(I32).rearrange("e p c -> p e c"))
 
-        for plane in (w1sc, w2sc):
-            nc.gpsimd.memset(plane[:, : E // 2, :].bitcast(I32), 0)
-            nc.vector.memset(plane[:, E // 2 :, :].bitcast(I32), 0)
+        def of_expert(tiles, groups, e):
+            for tile, (a, b) in zip(tiles, groups):
+                if a <= e < b:
+                    return tile, e - a
+
+        nc.gpsimd.memset(v1sc[:].bitcast(I32), 0)
         make_identity(nc, ident[:])
 
-        nc.sync.dma_start(offsets[:], offs)
-        load_full_plane(nc.sync, xs, x_scales)
-        nc.sync.dma_start(out=xw[:].bitcast(I32), in_=x_words[0].rearrange("p t d -> p (t d)").bitcast(I32))
-        load_w1(nc.sync, 0)
-        load_expert_planes(nc.sync, w1sc, w1_scales)
-        load_w1(nc.sync, 1)
-        nc.sync.dma_start(out=v1w[:], in_=w1s_words[0].rearrange("p l d -> p (l d)").bitcast(I32))
-        load_full_plane(nc.sync, v1sc, w1s_scales)
-        nc.sync.dma_start(out=w2w[:].bitcast(I32), in_=w2_words[:, 0].bitcast(I32).rearrange("e p c -> p e c"))
-        load_expert_planes(nc.sync, w2sc, w2_scales)
-        load_w1(nc.sync, 2)
-        nc.sync.dma_start(out=g[:], in_=gate)
-        nc.sync.dma_start(out=v2w[:], in_=w2s_words[0].rearrange("p n d -> p (n d)").bitcast(I32))
-        load_full_plane(nc.sync, v2sc, w2s_scales)
 
-        slot_words, slot_scales, w1_of = {}, {}, {}
+        nc.sync.dma_start(offsets[:], offs)
+        for q in range(4):
+            load_full_plane(nc.sync if q % 2 else nc.scalar, xs, x_scales, q)
+        nc.sync.dma_start(out=xw[:].bitcast(I32), in_=x_words[0].rearrange("p t d -> p (t d)").bitcast(I32))
+        load_words(nc.sync, w1w[0], w1_words, *W1_GROUPS[0])
+        for r in range(4):
+            load_expert_planes(nc.sync, w1sc, w1_scales, r)
+        load_words(nc.sync, w1w[1], w1_words, *W1_GROUPS[1])
+        nc.sync.dma_start(out=v1w[:], in_=w1s_words[0].rearrange("p l d -> p (l d)").bitcast(I32))
+        load_expert_planes(nc.sync, w2sc, w2_scales, 0)
+        load_words(nc.sync, w2w[0], w2_words, *W2_GROUPS[0])
+        for r in range(1, 4):
+            load_expert_planes(nc.sync, w2sc, w2_scales, r)
+        load_plane(nc.sync, v1sc, w1s_scales, 0)
+        for r in range(1, 4):
+            load_plane(nc.sync, v1sc, w1s_scales, r)
+        load_words(nc.sync, w1w[2], w1_words, *W1_GROUPS[2])
+        nc.sync.dma_start(out=g[0][:], in_=gate[:, : 2 * C])
+        load_words(nc.sync, w2w[1], w2_words, *W2_GROUPS[1])
+        nc.sync.dma_start(out=g[1][:], in_=gate[:, 2 * C :])
+        nc.sync.dma_start(out=v2w[:], in_=w2s_words[0].rearrange("p n d -> p (n d)").bitcast(I32))
+        for r in range(4):
+            load_plane(nc.sync, v2sc, w2s_scales, r)
+
+        slot_words, slot_scales = {}, {}
 
         def gather(i):
             a, b = GATHER_GROUPS[i]
@@ -106,14 +121,14 @@ def tile_moe_shf_mlp_gelu_kernel(
             for e in range(a, b):
                 slot_words[e] = words[:, (e - a) * C : (e - a + 1) * C]
                 slot_scales[e] = scales[:, (e - a) * C : (e - a + 1) * C]
-                w1_of[e] = w1w[i][:, e - a, :]
 
         h_codes = {}
+        ykeep = {}
 
         def halves(e):
             return (slice(0, 1), slice(1, 2)) if e == 0 else (slice(0, 2),)
 
-        def activate(pre, words, scales, w, w_scales, turned, parts):
+        def activate(pre, words, scales, w, w_scales, parts):
             nc.tensor.matmul_mx(
                 out=pre[:], lhsT=words.bitcast(FP8X4), lhsT_scale=scales, rhs=w, rhs_scale=w_scales,
                 start=True, stop=True,
@@ -124,59 +139,87 @@ def tile_moe_shf_mlp_gelu_kernel(
                     out=h_rows[:].rearrange("s (u p v) -> s u p v", u=2, v=2)[:, u],
                     in_=pre[:].rearrange("s (p u v) -> s u p v", u=2, v=2)[:, u], func=GELU,
                 )
-            pairs = h_rows[:].bitcast(F32)
-            for u in range(2):
-                nc.tensor.transpose(turned[:, u, :], pairs[:, u * P : (u + 1) * P], ident[:])
+            return h_rows
 
-        routed_turned = {}
+        routed_turned, routed_rows = {}, {}
+
+        def routed_turn(e):
+            pairs = routed_rows[e][:].bitcast(F32)
+            for u in range(2):
+                nc.tensor.transpose(routed_turned[e][:, u, :], pairs[:, u * P : (u + 1) * P], ident[:])
 
         def routed_activate(e):
             routed_turned[e] = bank[ROUTED_TURN[e]][:, : 2 * C].rearrange("p (u s) -> p u s", u=2)
-            activate(
-                bank[ROUTED_PRE[e]], slot_words[e], slot_scales[e], w1_of[e].bitcast(FP4X4), w1sc[:, e, :],
-                routed_turned[e], halves(e),
+            w1_tile, place = of_expert(w1w, W1_GROUPS, e)
+            routed_rows[e] = activate(
+                bank[ROUTED_PRE[e]], slot_words[e], slot_scales[e], w1_tile[:, place, :].bitcast(FP4X4), w1sc[:, e, :],
+                halves(e),
             )
+            if e not in (2, 3):
+                routed_turn(e)
 
-        def routed_quantize(e):
+        h_ins = {}
+
+        def routed_interleave(e):
             h_in = ring.tile([P, C * PACK], BF16, name="h_in", align_bytes=64)
-            nc.scalar.copy(
+            copy = nc.vector.tensor_copy if e < 2 else nc.scalar.copy
+            copy(
                 out=h_in[:].bitcast(F32).rearrange("p (s u) -> p s u", u=2),
                 in_=routed_turned[e].rearrange("p u s -> p s u"),
             )
-            codes = ring.tile([P, C], U32, name="h_codes", align_bytes=64)
+            h_ins[e] = h_in
+
+        def routed_quantize(e):
+            if e < 2:
+                routed_interleave(e)
+            h_in = h_ins[e]
+            if e >= 2:
+                codes = keep.tile([P, C], U32, name="h_codes_late", tag="y%d_0" % (e - 2), align_bytes=64)
+            else:
+                codes = ring.tile([P, C], U32, name="h_codes", align_bytes=64)
             scales = ring.tile([P, C], U8, name="h_scales", align_bytes=64)
             nc.vector.quantize_mx(out=codes[:].bitcast(FP8X4), scales=scales[:], in_=h_in[:])
             h_codes[e] = (codes, scales)
 
         def routed_second(e):
             codes, scales = h_codes[e]
-            y = bank[ROUTED_Y[e]][:, : NB * C].rearrange("p (b s) -> p b s", b=NB)
+            w2_tile, place = of_expert(w2w, W2_GROUPS, e)
+            g_tile, place = of_expert(g, W2_GROUPS, e)
+            y = [bank[ROUTED_Y[e][nb]][:, nb * C : (nb + 1) * C] for nb in range(NB)]
             for nb in range(NB):
                 nc.tensor.matmul_mx(
-                    out=y[:, nb, :], lhsT=w2w[:, e, 2 * nb * P : 2 * (nb + 1) * P].bitcast(FP4X4),
+                    out=y[nb], lhsT=w2_tile[:, place, 2 * nb * P : 2 * (nb + 1) * P].bitcast(FP4X4),
                     lhsT_scale=w2sc[:, e, nb * P : (nb + 1) * P],
                     rhs=codes[:].bitcast(FP8X4), rhs_scale=scales[:], start=True, stop=True,
                 )
-            y_sb = keep.tile([P, NB, C], F32, name="y_sb%d" % e)
-            for nb in halves(e):
-                nc.scalar.copy(out=y_sb[:, nb], in_=y[:, nb])
+            if e + 2 < E:
+                y_sb = [keep.tile([P, C], F32, name="y", tag="y%d_%d" % (e, nb), align_bytes=64)[:] for nb in range(NB)]
+                for nb in range(NB):
+                    nc.scalar.copy(out=y_sb[nb], in_=y[nb])
+            else:
+                both = keep.tile([P, NB, C], F32, name="y_sb%d" % e)
+                nc.scalar.copy(out=both[:].rearrange("p b s -> p (b s)"), in_=bank[ROUTED_Y[e][0]][:, : NB * C])
+                y_sb = [both[:, nb, :] for nb in range(NB)]
+            ykeep[e] = y_sb
             for nb in range(NB):
                 nc.vector.tensor_tensor(
                     out=win[nb][:].indirect(offsets[:, e * C // 16 : (e + 1) * C // 16]),
-                    in0=y_sb[:, nb, :], in1=g[:, e * C : (e + 1) * C], op=MULT,
+                    in0=y_sb[nb], in1=g_tile[:, place * C : (place + 1) * C], op=MULT,
                 )
 
         ys = {}
-        hs_in = [keep.tile([P, CHUNK * PACK], BF16, name="hs_in%d" % c, align_bytes=64) for c in range(T // CHUNK)]
+        for nb in range(NB):
+            ys[0, nb] = bank[3][:, nb * 256 : (nb + 1) * 256]
+            ys[1, nb] = bank[nb][:]
+        hs_in = [keep.tile([P, (b - a) * PACK], BF16, name="hs_in%d" % a, align_bytes=64) for a, b in CHUNKS]
 
-        def permute_shared():
-            words = keep.tile([P, HS], I32, name="v1w_perm", tag="xgw0", align_bytes=64)
-            scales = slots.tile([P, HS], U8, name="v1sc_perm", tag="plane", align_bytes=64)
-            for dest, src in ((words, v1w), (scales, v1sc)):
-                nc.vector.tensor_copy(
-                    out=dest[:].rearrange("p (d m) -> p d m", d=PACK), in_=src[:].rearrange("p (m d) -> p d m", d=PACK)
-                )
-            return words, scales
+        def permute(src, dtype, run):
+            dest = keep.tile([P, HS], dtype, name="perm%d" % run, align_bytes=64)
+            nc.vector.tensor_copy(
+                out=dest[:].rearrange("p (d a b) -> p a d b", d=PACK, b=run),
+                in_=src[:].rearrange("p (a b d) -> p a d b", d=PACK, b=run),
+            )
+            return dest
 
         def shared_activate(tb):
             pre = bank[SHARED_PRE[tb]][:].rearrange("p (d t) -> p d t", d=PACK)
@@ -187,51 +230,75 @@ def tile_moe_shf_mlp_gelu_kernel(
                     lhsT_scale=v1sc_perm[:, d * P : (d + 1) * P],
                     rhs=xw[:, cols].bitcast(FP8X4), rhs_scale=xs[:, cols], start=True, stop=True,
                 )
-            c, half = divmod(tb, 2)
+            c = min(tb // 2, 1)
+            half = tb - 2 * c
             nc.scalar.activation(
                 out=hs_in[c][:, half * P * PACK : (half + 1) * P * PACK].rearrange("p (t d) -> p t d", d=PACK),
                 in_=pre.rearrange("p d t -> p t d"), func=GELU,
             )
 
         def shared_second(c):
-            codes = keep.tile([P, CHUNK], U32, name="hs_codes%d" % c, align_bytes=64)
-            scales = keep.tile([P, CHUNK], U8, name="hs_scales%d" % c, align_bytes=64)
+            width = CHUNKS[c][1] - CHUNKS[c][0]
+            codes = keep.tile([P, width], U32, name="hs_codes", tag=("y1_1", "hs_codes")[c], align_bytes=64)
+            scales = keep.tile([P, width], U8, name="hs_scales%d" % c, align_bytes=64)
             nc.vector.quantize_mx(out=codes[:].bitcast(FP8X4), scales=scales[:], in_=hs_in[c][:])
-            ys[c] = bank[SHARED_Y[c]][:].rearrange("p (b t) -> p b t", b=NB)
             for nb in range(NB):
                 nc.tensor.matmul_mx(
-                    out=ys[c][:, nb, :], lhsT=v2w[:, nb * P : (nb + 1) * P].bitcast(FP8X4),
+                    out=ys[c, nb], lhsT=v2w[:, nb * P : (nb + 1) * P].bitcast(FP8X4),
                     lhsT_scale=v2sc[:, nb * P : (nb + 1) * P],
                     rhs=codes[:].bitcast(FP8X4), rhs_scale=scales[:], start=True, stop=True,
                 )
 
-        def finish(c, nb):
-            cols = slice(c * CHUNK, (c + 1) * CHUNK)
-            res = keep.tile([P, CHUNK], F32, name="res%d_%d" % (nb, c))
-            nc.vector.tensor_tensor(out=res[:], in0=ys[c][:, nb, :], in1=win[nb][:, cols], op=ADD)
+        def finish(nb, cols, sums):
+            res = keep.tile([P, cols.stop - cols.start], F32, name="res%d_%d" % (nb, cols.start))
+            if (nb, cols.start) == (0, 256):
+                moved = keep.tile([P, cols.stop - cols.start], F32, name="ys_moved")
+                nc.scalar.copy(out=moved[:], in_=sums)
+                nc.gpsimd.tensor_tensor(out=res[:], in0=moved[:], in1=win[nb][:, cols], op=ADD)
+            else:
+                nc.vector.tensor_tensor(out=res[:], in0=sums, in1=win[nb][:, cols], op=ADD)
             nc.sync.dma_start(out=out[nb * P : (nb + 1) * P, cols], in_=res[:])
 
         gather(0)
+        for i in range(5):
+            nc.tensor.matmul_mx(
+                out=bank[5][:, :C], lhsT=slot_words[0].bitcast(FP8X4), lhsT_scale=slot_scales[0],
+                rhs=slot_words[0].bitcast(FP8X4), rhs_scale=slot_scales[0], start=True, stop=True,
+            )
         gather(1)
         routed_activate(0)
-        routed_activate(1)
-        routed_quantize(0)
         gather(2)
+        routed_activate(1)
+        v1w_perm = permute(v1w, I32, 4)
+        routed_quantize(0)
         routed_quantize(1)
+        v1sc_perm = permute(v1sc, U8, 16)
         routed_activate(2)
-        v1w_perm, v1sc_perm = permute_shared()
+        routed_activate(3)
         routed_second(0)
-        for e in range(1, E):
-            if e + 1 < E:
-                routed_quantize(e + 1)
-            if e + 2 < E:
-                routed_activate(e + 2)
-            shared_activate(e - 1)
-            if e == E - 1:
-                shared_activate(e)
-            routed_second(e)
-        for c in range(T // CHUNK):
-            shared_second(c)
-        for c in range(T // CHUNK):
-            for nb in range(NB):
-                finish(c, nb)
+        routed_turn(2)
+        routed_second(1)
+        routed_turn(3)
+        routed_interleave(2)
+        routed_quantize(2)
+        routed_interleave(3)
+        routed_quantize(3)
+        routed_activate(4)
+        routed_second(2)
+        routed_interleave(4)
+        routed_quantize(4)
+        routed_activate(5)
+        routed_second(3)
+        routed_interleave(5)
+        routed_quantize(5)
+        for tb in range(3):
+            shared_activate(tb)
+        shared_second(0)
+        routed_second(4)
+        for tb in range(3, 6):
+            shared_activate(tb)
+        shared_second(1)
+        routed_second(5)
+        for nb in range(NB):
+            for c in (1, 0):
+                finish(nb, slice(*CHUNKS[c]), ys[c, nb])

@@ -15,20 +15,23 @@ U8 = mybir.dt.uint8
 FP8X4 = mybir.dt.float8_e4m3fn_x4
 FP4X4 = mybir.dt.float4_e2m1fn_x4
 GELU = mybir.ActivationFunctionType.Gelu_apprx_tanh
+COPY = mybir.ActivationFunctionType.Copy
 MULT = mybir.AluOpType.mult
 ADD = mybir.AluOpType.add
 
 P = 128
 PACK = 4
 NB = N // P
-CHUNKS = ((0, 256), (256, 768))
-ROUTED_PRE = (0, 1, 0, 1, 0, 7)
-ROUTED_TURN = (2, 3, 7, 4, 2, 3)
-ROUTED_Y = ((7, 7), (4, 4), (7, 4), (2, 2), (5, 5), (4, 4))
-SHARED_PRE = (5, 6, 5, 6, 4, 6)
-W1_GROUPS = ((0, 2), (2, 4), (4, 6))
-W2_GROUPS = ((0, 2), (2, 6))
-GATHER_GROUPS = ((0, 1), (1, 3), (3, 6))
+PAIRS = E // 2
+CHUNKS = ((0, 256), (256, 512), (512, 768))
+W1_GROUPS = ((0, 2), (2, 6))
+WORD_GROUPS = ((0, 1), (1, 2), (2, 4), (4, 6))
+SCALE_GROUPS = ((0, 1), (1, 4), (4, 6))
+ROUTED_PRE = (0, 1, 2, 0, 1, 2)
+TURNED = (3, 4, 6)
+ROUTED_Y = ((5, 6), (0, 1), (3, 4))
+SHARED_PRE = (7, 5, 6, 1, 5, 0)
+SHARED_Y = (2, 7, 6)
 
 
 def tile_moe_shf_mlp_gelu_kernel(
@@ -38,8 +41,7 @@ def tile_moe_shf_mlp_gelu_kernel(
     nc = tc.nc
     with ExitStack() as ctx:
         keep = ctx.enter_context(tc.tile_pool(name="keep", bufs=1))
-        ring = ctx.enter_context(tc.tile_pool(name="ring", bufs=6))
-        slots = ctx.enter_context(tc.tile_pool(name="slots", bufs=2))
+        reuse = ctx.enter_context(tc.tile_pool(name="reuse", bufs=1))
         psum = ctx.enter_context(tc.psum_pool(name="psum", bufs=1))
         bank = [psum.tile([P, 512], F32, name="bank%d" % i) for i in range(8)]
 
@@ -48,19 +50,21 @@ def tile_moe_shf_mlp_gelu_kernel(
         xs = keep.tile([P, T], U8, name="xs", align_bytes=64)
         w1w = [keep.tile([P, b - a, 2 * H], U8, name="w1w%d" % a, align_bytes=64) for a, b in W1_GROUPS]
         w1sc = keep.tile([P, E, H], U8, name="w1sc", align_bytes=64)
-        w2w = [keep.tile([P, b - a, 2 * N], U8, name="w2w%d" % a, align_bytes=64) for a, b in W2_GROUPS]
+        w2w = keep.tile([P, E, 2 * N], U8, name="w2w", align_bytes=64)
         w2sc = keep.tile([P, E, N], U8, name="w2sc", align_bytes=64)
         v1w = keep.tile([P, HS], I32, name="v1w", align_bytes=64)
-        v1sc = keep.tile([P, HS], U8, name="v1sc", align_bytes=64)
+        v1sc = reuse.tile([P, HS], U8, name="v1sc", align_bytes=64, offset=0)
         v2w = keep.tile([P, N], I32, name="v2w", align_bytes=64)
         v2sc = keep.tile([P, N], U8, name="v2sc", align_bytes=64)
-        g = [keep.tile([P, (b - a) * C], F32, name="g%d" % a) for a, b in W2_GROUPS]
+        g_first = reuse.tile([P, 2 * C], F32, name="g_first", align_bytes=64, offset=4 * HS)
+        g_rest = keep.tile([P, 4 * C], F32, name="g_rest")
+        g = [g_first[:], g_rest[:, : 2 * C], g_rest[:, 2 * C :]]
         ident = keep.tile([P, P], F32, name="ident")
         win = [keep.tile([P, T], F32, name="win%d" % nb) for nb in range(NB)]
 
-        def load_plane(queue, plane, scales, r):
+        def load_plane(plane, scales, r):
             rows = scales[0].bitcast(I32).rearrange("(q r) c -> r q c", r=4)
-            queue.dma_start(out=plane[:].bitcast(I32)[r:P:32], in_=rows[r])
+            nc.sync.dma_start(out=plane[:].bitcast(I32)[r:P:32], in_=rows[r])
 
         def load_full_plane(queue, plane, scales, q):
             rows = scales[0].bitcast(I32).rearrange("(q r) c -> q r c", r=4)
@@ -69,149 +73,137 @@ def tile_moe_shf_mlp_gelu_kernel(
                 in_=rows[q].unsqueeze(0).to_broadcast([8, 4, rows.shape[2]]),
             )
 
-        def load_expert_planes(queue, plane, scales, r):
+        def load_expert_planes(plane, scales, r):
             rows = scales[:, 0].bitcast(I32).rearrange("e (q r) c -> r q e c", r=4)
-            queue.dma_start(out=plane[:].bitcast(I32)[r:P:32], in_=rows[r])
+            nc.sync.dma_start(out=plane[:].bitcast(I32)[r:P:32], in_=rows[r])
 
-        def load_words(queue, tile, words, a, b):
-            queue.dma_start(out=tile[:].bitcast(I32), in_=words[a:b, 0].bitcast(I32).rearrange("e p c -> p e c"))
-
-        def of_expert(tiles, groups, e):
-            for tile, (a, b) in zip(tiles, groups):
-                if a <= e < b:
-                    return tile, e - a
+        def load_words(tile, words, a, b):
+            nc.sync.dma_start(out=tile[:].bitcast(I32), in_=words[a:b, 0].bitcast(I32).rearrange("e p c -> p e c"))
 
         nc.gpsimd.memset(v1sc[:].bitcast(I32), 0)
         make_identity(nc, ident[:])
-
 
         nc.sync.dma_start(offsets[:], offs)
         for q in range(4):
             load_full_plane(nc.sync if q % 2 else nc.scalar, xs, x_scales, q)
         nc.sync.dma_start(out=xw[:].bitcast(I32), in_=x_words[0].rearrange("p t d -> p (t d)").bitcast(I32))
-        load_words(nc.sync, w1w[0], w1_words, *W1_GROUPS[0])
+        load_words(w1w[0], w1_words, *W1_GROUPS[0])
+        load_plane(v1sc, w1s_scales, 0)
         for r in range(4):
-            load_expert_planes(nc.sync, w1sc, w1_scales, r)
-        load_words(nc.sync, w1w[1], w1_words, *W1_GROUPS[1])
+            load_expert_planes(w1sc, w1_scales, r)
+        load_words(w1w[1], w1_words, *W1_GROUPS[1])
         nc.sync.dma_start(out=v1w[:], in_=w1s_words[0].rearrange("p l d -> p (l d)").bitcast(I32))
-        load_expert_planes(nc.sync, w2sc, w2_scales, 0)
-        load_words(nc.sync, w2w[0], w2_words, *W2_GROUPS[0])
         for r in range(1, 4):
-            load_expert_planes(nc.sync, w2sc, w2_scales, r)
-        load_plane(nc.sync, v1sc, w1s_scales, 0)
-        for r in range(1, 4):
-            load_plane(nc.sync, v1sc, w1s_scales, r)
-        load_words(nc.sync, w1w[2], w1_words, *W1_GROUPS[2])
-        nc.sync.dma_start(out=g[0][:], in_=gate[:, : 2 * C])
-        load_words(nc.sync, w2w[1], w2_words, *W2_GROUPS[1])
-        nc.sync.dma_start(out=g[1][:], in_=gate[:, 2 * C :])
+            load_plane(v1sc, w1s_scales, r)
+        load_words(w2w, w2_words, 0, E)
+        for r in range(4):
+            load_expert_planes(w2sc, w2_scales, r)
+        nc.sync.dma_start(out=g_first[:], in_=gate[:, : 2 * C])
+        nc.sync.dma_start(out=g_rest[:], in_=gate[:, 2 * C :])
         nc.sync.dma_start(out=v2w[:], in_=w2s_words[0].rearrange("p n d -> p (n d)").bitcast(I32))
         for r in range(4):
-            load_plane(nc.sync, v2sc, w2s_scales, r)
+            load_plane(v2sc, w2s_scales, r)
 
         slot_words, slot_scales = {}, {}
 
-        def gather(i):
-            a, b = GATHER_GROUPS[i]
-            words = keep.tile([P, (b - a) * C], U32, name="xgw", tag="xgw%d" % i, align_bytes=64)
-            scales = slots.tile([P, (b - a) * C], U8, name="xgs", tag="plane", align_bytes=64)
-            piece = offsets[:, a * C // 16 : b * C // 16]
-            nc.vector.tensor_copy(out=words[:], in_=xw[:].indirect(piece))
-            nc.vector.tensor_copy(out=scales[:], in_=xs[:].indirect(piece))
+        def gather_words(a, b):
+            words = keep.tile([P, (b - a) * C], U32, name="xgw%d" % a, align_bytes=64)
+            nc.vector.tensor_copy(out=words[:], in_=xw[:].indirect(offsets[:, a * C // 16 : b * C // 16]))
             for e in range(a, b):
                 slot_words[e] = words[:, (e - a) * C : (e - a + 1) * C]
+
+        def gather_scales(a, b):
+            place = HS + 2 * C if a == 1 else HS
+            scales = reuse.tile([P, (b - a) * C], U8, name="xgs%d" % a, align_bytes=64, offset=place)
+            nc.vector.tensor_copy(out=scales[:], in_=xs[:].indirect(offsets[:, a * C // 16 : b * C // 16]))
+            for e in range(a, b):
                 slot_scales[e] = scales[:, (e - a) * C : (e - a + 1) * C]
 
-        h_codes = {}
-        ykeep = {}
+        def turned(pair):
+            return bank[TURNED[pair]][:].rearrange("p (e u s) -> p e u s", e=2, u=2)
 
-        def halves(e):
-            return (slice(0, 1), slice(1, 2)) if e == 0 else (slice(0, 2),)
-
-        def activate(pre, words, scales, w, w_scales, parts):
-            nc.tensor.matmul_mx(
-                out=pre[:], lhsT=words.bitcast(FP8X4), lhsT_scale=scales, rhs=w, rhs_scale=w_scales,
-                start=True, stop=True,
-            )
-            h_rows = ring.tile([P, H], BF16, name="h_rows", align_bytes=64)
-            for u in parts:
-                nc.scalar.activation(
-                    out=h_rows[:].rearrange("s (u p v) -> s u p v", u=2, v=2)[:, u],
-                    in_=pre[:].rearrange("s (p u v) -> s u p v", u=2, v=2)[:, u], func=GELU,
-                )
-            return h_rows
-
-        routed_turned, routed_rows = {}, {}
-
-        def routed_turn(e):
-            pairs = routed_rows[e][:].bitcast(F32)
-            for u in range(2):
-                nc.tensor.transpose(routed_turned[e][:, u, :], pairs[:, u * P : (u + 1) * P], ident[:])
+        h_rows = {}
 
         def routed_activate(e):
-            routed_turned[e] = bank[ROUTED_TURN[e]][:, : 2 * C].rearrange("p (u s) -> p u s", u=2)
-            w1_tile, place = of_expert(w1w, W1_GROUPS, e)
-            routed_rows[e] = activate(
-                bank[ROUTED_PRE[e]], slot_words[e], slot_scales[e], w1_tile[:, place, :].bitcast(FP4X4), w1sc[:, e, :],
-                halves(e),
+            group = 0 if e < W1_GROUPS[0][1] else 1
+            w = w1w[group][:, e - W1_GROUPS[group][0], :]
+            pre = bank[ROUTED_PRE[e]]
+            nc.tensor.matmul_mx(
+                out=pre[:], lhsT=slot_words[e].bitcast(FP8X4), lhsT_scale=slot_scales[e],
+                rhs=w.bitcast(FP4X4), rhs_scale=w1sc[:, e, :], start=True, stop=True,
             )
-            if e not in (2, 3):
-                routed_turn(e)
+            h_rows[e] = keep.tile([P, H], BF16, name="h_rows%d" % e, align_bytes=64)
+            nc.scalar.activation(
+                out=h_rows[e][:].rearrange("s (u p v) -> s u p v", u=2, v=2),
+                in_=pre[:].rearrange("s (p u v) -> s u p v", u=2, v=2), func=GELU,
+            )
 
-        h_ins = {}
+        def routed_turn(e):
+            pairs = h_rows[e][:].bitcast(F32)
+            for u in range(2):
+                nc.tensor.transpose(turned(e // 2)[:, e % 2, u, :], pairs[:, u * P : (u + 1) * P], ident[:])
 
-        def routed_interleave(e):
-            h_in = ring.tile([P, C * PACK], BF16, name="h_in", align_bytes=64)
-            copy = nc.vector.tensor_copy if e < 2 else nc.scalar.copy
+        def routed_first(e):
+            routed_activate(e)
+            routed_turn(e)
+
+        h_in, h_codes, gated = {}, {}, {}
+
+        def routed_interleave(pair, copy):
+            if pair == 2:
+                h_in[pair] = reuse.tile([P, 2 * C * PACK], BF16, name="h_in2", align_bytes=64, offset=8 * HS)
+            else:
+                h_in[pair] = keep.tile([P, 2 * C * PACK], BF16, name="h_in%d" % pair, align_bytes=64)
             copy(
-                out=h_in[:].bitcast(F32).rearrange("p (s u) -> p s u", u=2),
-                in_=routed_turned[e].rearrange("p u s -> p s u"),
+                out=h_in[pair][:].bitcast(F32).rearrange("p (e s u) -> p e s u", e=2, u=2),
+                in_=turned(pair).rearrange("p e u s -> p e s u"),
             )
-            h_ins[e] = h_in
 
-        def routed_quantize(e):
-            if e < 2:
-                routed_interleave(e)
-            h_in = h_ins[e]
-            if e >= 2:
-                codes = keep.tile([P, C], U32, name="h_codes_late", tag="y%d_0" % (e - 2), align_bytes=64)
+        def routed_quantize(pair):
+            if pair == 1:
+                codes = reuse.tile([P, 2 * C], U32, name="h_codes1", align_bytes=64, offset=4 * HS)
             else:
-                codes = ring.tile([P, C], U32, name="h_codes", align_bytes=64)
-            scales = ring.tile([P, C], U8, name="h_scales", align_bytes=64)
-            nc.vector.quantize_mx(out=codes[:].bitcast(FP8X4), scales=scales[:], in_=h_in[:])
-            h_codes[e] = (codes, scales)
+                codes = keep.tile([P, 2 * C], U32, name="h_codes%d" % pair, align_bytes=64)
+            if pair == 0:
+                scales = reuse.tile([P, 2 * C], U8, name="h_scales0", align_bytes=64, offset=0)
+            else:
+                scales = keep.tile([P, 2 * C], U8, name="h_scales%d" % pair, align_bytes=64)
+            nc.vector.quantize_mx(out=codes[:].bitcast(FP8X4), scales=scales[:], in_=h_in[pair][:])
+            h_codes[pair] = (codes, scales)
 
-        def routed_second(e):
-            codes, scales = h_codes[e]
-            w2_tile, place = of_expert(w2w, W2_GROUPS, e)
-            g_tile, place = of_expert(g, W2_GROUPS, e)
-            y = [bank[ROUTED_Y[e][nb]][:, nb * C : (nb + 1) * C] for nb in range(NB)]
-            for nb in range(NB):
+        def routed_second(pair, nb):
+            codes, scales = h_codes[pair]
+            for i in range(2):
+                e = 2 * pair + i
                 nc.tensor.matmul_mx(
-                    out=y[nb], lhsT=w2_tile[:, place, 2 * nb * P : 2 * (nb + 1) * P].bitcast(FP4X4),
+                    out=bank[ROUTED_Y[pair][nb]][:, i * C : (i + 1) * C],
+                    lhsT=w2w[:, e, 2 * nb * P : 2 * (nb + 1) * P].bitcast(FP4X4),
                     lhsT_scale=w2sc[:, e, nb * P : (nb + 1) * P],
-                    rhs=codes[:].bitcast(FP8X4), rhs_scale=scales[:], start=True, stop=True,
-                )
-            if e + 2 < E:
-                y_sb = [keep.tile([P, C], F32, name="y", tag="y%d_%d" % (e, nb), align_bytes=64)[:] for nb in range(NB)]
-                for nb in range(NB):
-                    nc.scalar.copy(out=y_sb[nb], in_=y[nb])
-            else:
-                both = keep.tile([P, NB, C], F32, name="y_sb%d" % e)
-                nc.scalar.copy(out=both[:].rearrange("p b s -> p (b s)"), in_=bank[ROUTED_Y[e][0]][:, : NB * C])
-                y_sb = [both[:, nb, :] for nb in range(NB)]
-            ykeep[e] = y_sb
-            for nb in range(NB):
-                nc.vector.tensor_tensor(
-                    out=win[nb][:].indirect(offsets[:, e * C // 16 : (e + 1) * C // 16]),
-                    in0=y_sb[nb], in1=g_tile[:, place * C : (place + 1) * C], op=MULT,
+                    rhs=codes[:, i * C : (i + 1) * C].bitcast(FP8X4), rhs_scale=scales[:, i * C : (i + 1) * C],
+                    start=True, stop=True,
                 )
 
-        ys = {}
-        for nb in range(NB):
-            ys[0, nb] = bank[3][:, nb * 256 : (nb + 1) * 256]
-            ys[1, nb] = bank[nb][:]
-        hs_in = [keep.tile([P, (b - a) * PACK], BF16, name="hs_in%d" % a, align_bytes=64) for a, b in CHUNKS]
+        def routed_gate(a, b, nb, place=None):
+            name = "gated%d_%d" % (a, nb)
+            if place is None:
+                gated[a, nb] = keep.tile([P, (b - a) * C], F32, name=name)
+            else:
+                gated[a, nb] = reuse.tile([P, (b - a) * C], F32, name=name, align_bytes=64, offset=place)
+            cols = slice(a % 2 * C, (a % 2 + b - a) * C)
+            nc.vector.tensor_tensor(
+                out=gated[a, nb][:], in0=bank[ROUTED_Y[a // 2][nb]][:, cols], in1=g[a // 2][:, cols], op=MULT
+            )
+
+        def scatter(a, b, nb):
+            places = win[nb][:].indirect(offsets[:, a * C // 16 : b * C // 16])
+            if nb == 0:
+                nc.vector.tensor_copy(out=places, in_=gated[a, nb][:])
+            else:
+                nc.scalar.activation(out=places, in_=gated[a, nb][:], func=COPY)
+
+        ys = {(c, nb): bank[SHARED_Y[c]][:, nb * 256 : (nb + 1) * 256] for c in range(3) for nb in range(NB)}
+        hs_in = [keep.tile([P, (b - a) * PACK], BF16, name="hs_in%d" % a, align_bytes=64) for a, b in CHUNKS[:2]]
+        hs_in.append(reuse.tile([P, 256 * PACK], BF16, name="hs_in_last", align_bytes=64, offset=12 * HS))
 
         def permute(src, dtype, run):
             dest = keep.tile([P, HS], dtype, name="perm%d" % run, align_bytes=64)
@@ -221,7 +213,7 @@ def tile_moe_shf_mlp_gelu_kernel(
             )
             return dest
 
-        def shared_activate(tb):
+        def shared_first(tb):
             pre = bank[SHARED_PRE[tb]][:].rearrange("p (d t) -> p d t", d=PACK)
             cols = slice(tb * P, (tb + 1) * P)
             for d in range(PACK):
@@ -230,18 +222,24 @@ def tile_moe_shf_mlp_gelu_kernel(
                     lhsT_scale=v1sc_perm[:, d * P : (d + 1) * P],
                     rhs=xw[:, cols].bitcast(FP8X4), rhs_scale=xs[:, cols], start=True, stop=True,
                 )
-            c = min(tb // 2, 1)
-            half = tb - 2 * c
+            c = tb * P // CHUNKS[1][0]
+            place = tb * P - CHUNKS[c][0]
             nc.scalar.activation(
-                out=hs_in[c][:, half * P * PACK : (half + 1) * P * PACK].rearrange("p (t d) -> p t d", d=PACK),
+                out=hs_in[c][:, place * PACK : (place + P) * PACK].rearrange("p (t d) -> p t d", d=PACK),
                 in_=pre.rearrange("p d t -> p t d"), func=GELU,
             )
 
-        def shared_second(c):
+        hs_codes = {}
+
+        def shared_quantize(c):
             width = CHUNKS[c][1] - CHUNKS[c][0]
-            codes = keep.tile([P, width], U32, name="hs_codes", tag=("y1_1", "hs_codes")[c], align_bytes=64)
+            codes = keep.tile([P, width], U32, name="hs_codes%d" % c, align_bytes=64)
             scales = keep.tile([P, width], U8, name="hs_scales%d" % c, align_bytes=64)
             nc.vector.quantize_mx(out=codes[:].bitcast(FP8X4), scales=scales[:], in_=hs_in[c][:])
+            hs_codes[c] = (codes, scales)
+
+        def shared_second(c):
+            codes, scales = hs_codes[c]
             for nb in range(NB):
                 nc.tensor.matmul_mx(
                     out=ys[c, nb], lhsT=v2w[:, nb * P : (nb + 1) * P].bitcast(FP8X4),
@@ -249,56 +247,66 @@ def tile_moe_shf_mlp_gelu_kernel(
                     rhs=codes[:].bitcast(FP8X4), rhs_scale=scales[:], start=True, stop=True,
                 )
 
-        def finish(nb, cols, sums):
-            res = keep.tile([P, cols.stop - cols.start], F32, name="res%d_%d" % (nb, cols.start))
-            if (nb, cols.start) == (0, 256):
-                moved = keep.tile([P, cols.stop - cols.start], F32, name="ys_moved")
-                nc.scalar.copy(out=moved[:], in_=sums)
-                nc.gpsimd.tensor_tensor(out=res[:], in0=moved[:], in1=win[nb][:, cols], op=ADD)
+        def finish(nb, c):
+            cols = slice(*CHUNKS[c])
+            if c == 1:
+                res = reuse.tile([P, 256], F32, name="res%d_1" % nb, align_bytes=64, offset=(12 + 2 * nb) * HS)
             else:
-                nc.vector.tensor_tensor(out=res[:], in0=sums, in1=win[nb][:, cols], op=ADD)
+                res = keep.tile([P, cols.stop - cols.start], F32, name="res%d_%d" % (nb, c))
+            nc.vector.tensor_tensor(out=res[:], in0=ys[c, nb], in1=win[nb][:, cols], op=ADD)
             nc.sync.dma_start(out=out[nb * P : (nb + 1) * P, cols], in_=res[:])
 
-        gather(0)
-        for i in range(5):
+        for i in range(2):
             nc.tensor.matmul_mx(
-                out=bank[5][:, :C], lhsT=slot_words[0].bitcast(FP8X4), lhsT_scale=slot_scales[0],
-                rhs=slot_words[0].bitcast(FP8X4), rhs_scale=slot_scales[0], start=True, stop=True,
+                out=bank[7][:], lhsT=xw[:, :P].bitcast(FP8X4), lhsT_scale=xs[:, :P],
+                rhs=xw[:, :512].bitcast(FP8X4), rhs_scale=xs[:, :512], start=True, stop=True,
             )
-        gather(1)
-        routed_activate(0)
-        gather(2)
-        routed_activate(1)
+        gather_scales(*SCALE_GROUPS[0])
+        gather_scales(*SCALE_GROUPS[1])
+        for a, b in WORD_GROUPS:
+            gather_words(a, b)
         v1w_perm = permute(v1w, I32, 4)
-        routed_quantize(0)
-        routed_quantize(1)
+        for e in range(4):
+            routed_first(e)
+        gather_scales(*SCALE_GROUPS[2])
         v1sc_perm = permute(v1sc, U8, 16)
-        routed_activate(2)
-        routed_activate(3)
-        routed_second(0)
-        routed_turn(2)
-        routed_second(1)
-        routed_turn(3)
-        routed_interleave(2)
-        routed_quantize(2)
-        routed_interleave(3)
-        routed_quantize(3)
+        routed_interleave(0, nc.vector.tensor_copy)
+        routed_quantize(0)
+        routed_second(0, 1)
+        routed_second(0, 0)
         routed_activate(4)
-        routed_second(2)
-        routed_interleave(4)
-        routed_quantize(4)
         routed_activate(5)
-        routed_second(3)
-        routed_interleave(5)
-        routed_quantize(5)
-        for tb in range(3):
-            shared_activate(tb)
+        routed_interleave(1, nc.vector.tensor_copy)
+        shared_first(0)
+        routed_gate(0, 2, 1)
+        routed_gate(0, 2, 0)
+        routed_quantize(1)
+        routed_second(1, 1)
+        routed_second(1, 0)
+        scatter(0, 2, 0)
+        scatter(0, 2, 1)
+        routed_turn(4)
+        routed_turn(5)
+        routed_interleave(2, nc.scalar.copy)
+        shared_first(1)
+        routed_gate(2, 4, 1)
+        routed_quantize(2)
+        routed_second(2, 1)
+        routed_second(2, 0)
+        routed_gate(2, 4, 0, 8 * HS)
+        scatter(2, 4, 0)
+        for tb in range(2, 6):
+            shared_first(tb)
+        routed_gate(4, 6, 1)
+        routed_gate(4, 6, 0)
+        scatter(2, 4, 1)
+        shared_quantize(0)
         shared_second(0)
-        routed_second(4)
-        for tb in range(3, 6):
-            shared_activate(tb)
-        shared_second(1)
-        routed_second(5)
-        for nb in range(NB):
-            for c in (1, 0):
-                finish(nb, slice(*CHUNKS[c]), ys[c, nb])
+        scatter(4, 6, 0)
+        scatter(4, 6, 1)
+        for c in range(len(CHUNKS)):
+            if c + 1 < len(CHUNKS):
+                shared_quantize(c + 1)
+                shared_second(c + 1)
+            for nb in range(NB):
+                finish(nb, c)

@@ -24,14 +24,14 @@ PACK = 4
 NB = N // P
 PAIRS = E // 2
 CHUNKS = ((0, 256), (256, 512), (512, 768))
-W1_GROUPS = ((0, 2), (2, 6))
+W1_GROUPS = ((0, 2), (2, 4), (4, 6))
 WORD_GROUPS = ((0, 1), (1, 2), (2, 4), (4, 6))
 SCALE_GROUPS = ((0, 1), (1, 4), (4, 6))
-ROUTED_PRE = (0, 1, 2, 0, 1, 2)
-TURNED = (3, 4, 6)
-ROUTED_Y = ((5, 6), (0, 1), (3, 4))
-SHARED_PRE = (7, 5, 6, 1, 5, 0)
-SHARED_Y = (2, 7, 6)
+ROUTED_PRE = ((0, 5), (1, 6), (2,), (5,), (6,), (2,))
+TURNED = (3, 4, 0, 0, 4, 4)
+ROUTED_Y = ((3, 4), (5, 6), (0, 1))
+SHARED_PRE = (7, 3, 4, 6, 3, 5)
+SHARED_Y = (2, 7, 4)
 
 
 def tile_moe_shf_mlp_gelu_kernel(
@@ -93,7 +93,9 @@ def tile_moe_shf_mlp_gelu_kernel(
             load_expert_planes(w1sc, w1_scales, r)
         load_words(w1w[1], w1_words, *W1_GROUPS[1])
         nc.sync.dma_start(out=v1w[:], in_=w1s_words[0].rearrange("p l d -> p (l d)").bitcast(I32))
-        for r in range(1, 4):
+        load_plane(v1sc, w1s_scales, 1)
+        load_words(w1w[2], w1_words, *W1_GROUPS[2])
+        for r in range(2, 4):
             load_plane(v1sc, w1s_scales, r)
         load_words(w2w, w2_words, 0, E)
         for r in range(4):
@@ -119,29 +121,33 @@ def tile_moe_shf_mlp_gelu_kernel(
             for e in range(a, b):
                 slot_scales[e] = scales[:, (e - a) * C : (e - a + 1) * C]
 
-        def turned(pair):
-            return bank[TURNED[pair]][:].rearrange("p (e u s) -> p e u s", e=2, u=2)
+        def turned(e):
+            return bank[TURNED[e]][:].rearrange("p (e u s) -> p e u s", e=2, u=2)
 
         h_rows = {}
 
         def routed_activate(e):
-            group = 0 if e < W1_GROUPS[0][1] else 1
-            w = w1w[group][:, e - W1_GROUPS[group][0], :]
-            pre = bank[ROUTED_PRE[e]]
-            nc.tensor.matmul_mx(
-                out=pre[:], lhsT=slot_words[e].bitcast(FP8X4), lhsT_scale=slot_scales[e],
-                rhs=w.bitcast(FP4X4), rhs_scale=w1sc[:, e, :], start=True, stop=True,
-            )
+            w = w1w[e // 2][:, e % 2, :]
+            pre = [bank[i] for i in ROUTED_PRE[e]]
             h_rows[e] = keep.tile([P, H], BF16, name="h_rows%d" % e, align_bytes=64)
-            nc.scalar.activation(
-                out=h_rows[e][:].rearrange("s (u p v) -> s u p v", u=2, v=2),
-                in_=pre[:].rearrange("s (p u v) -> s u p v", u=2, v=2), func=GELU,
-            )
+            parts = 2 if e < 2 else 1
+            width = H // parts
+            for a in range(0, H, width):
+                nc.tensor.matmul_mx(
+                    out=pre[a // width][:, a : a + width], lhsT=slot_words[e].bitcast(FP8X4), lhsT_scale=slot_scales[e],
+                    rhs=w[:, 2 * a : 2 * (a + width)].bitcast(FP4X4), rhs_scale=w1sc[:, e, a : a + width],
+                    start=True, stop=True,
+                )
+            for a in range(0, H, width):
+                nc.scalar.activation(
+                    out=h_rows[e][:].rearrange("s (u p v) -> s u p v", u=2, v=2)[:, :, a // PACK : (a + width) // PACK],
+                    in_=pre[a // width][:, a : a + width].rearrange("s (p u v) -> s u p v", u=2, v=2), func=GELU,
+                )
 
         def routed_turn(e):
             pairs = h_rows[e][:].bitcast(F32)
             for u in range(2):
-                nc.tensor.transpose(turned(e // 2)[:, e % 2, u, :], pairs[:, u * P : (u + 1) * P], ident[:])
+                nc.tensor.transpose(turned(e)[:, e % 2, u, :], pairs[:, u * P : (u + 1) * P], ident[:])
 
         def routed_first(e):
             routed_activate(e)
@@ -149,14 +155,15 @@ def tile_moe_shf_mlp_gelu_kernel(
 
         h_in, h_codes, gated = {}, {}, {}
 
-        def routed_interleave(pair, copy):
-            if pair == 2:
-                h_in[pair] = reuse.tile([P, 2 * C * PACK], BF16, name="h_in2", align_bytes=64, offset=8 * HS)
-            else:
-                h_in[pair] = keep.tile([P, 2 * C * PACK], BF16, name="h_in%d" % pair, align_bytes=64)
+        for pair in range(PAIRS - 1):
+            h_in[pair] = keep.tile([P, 2 * C * PACK], BF16, name="h_in%d" % pair, align_bytes=64)
+        h_in[2] = reuse.tile([P, 2 * C * PACK], BF16, name="h_in2", align_bytes=64, offset=8 * HS)
+
+        def routed_interleave(a, b, copy):
+            part = slice(a % 2, a % 2 + b - a)
             copy(
-                out=h_in[pair][:].bitcast(F32).rearrange("p (e s u) -> p e s u", e=2, u=2),
-                in_=turned(pair).rearrange("p e u s -> p e s u"),
+                out=h_in[a // 2][:].bitcast(F32).rearrange("p (e s u) -> p e s u", e=2, u=2)[:, part],
+                in_=turned(a).rearrange("p e u s -> p e s u")[:, part],
             )
 
         def routed_quantize(pair):
@@ -249,8 +256,8 @@ def tile_moe_shf_mlp_gelu_kernel(
 
         def finish(nb, c):
             cols = slice(*CHUNKS[c])
-            if c == 1:
-                res = reuse.tile([P, 256], F32, name="res%d_1" % nb, align_bytes=64, offset=(12 + 2 * nb) * HS)
+            if nb == 0 and c < 2:
+                res = reuse.tile([P, 256], F32, name="res0_%d" % c, align_bytes=64, offset=(12 + 2 * c) * HS)
             else:
                 res = keep.tile([P, cols.stop - cols.start], F32, name="res%d_%d" % (nb, c))
             nc.vector.tensor_tensor(out=res[:], in0=ys[c, nb], in1=win[nb][:, cols], op=ADD)
@@ -269,14 +276,15 @@ def tile_moe_shf_mlp_gelu_kernel(
         for e in range(4):
             routed_first(e)
         gather_scales(*SCALE_GROUPS[2])
+        routed_interleave(0, 1, nc.vector.tensor_copy)
+        routed_interleave(1, 2, nc.vector.tensor_copy)
         v1sc_perm = permute(v1sc, U8, 16)
-        routed_interleave(0, nc.vector.tensor_copy)
         routed_quantize(0)
         routed_second(0, 1)
         routed_second(0, 0)
         routed_activate(4)
         routed_activate(5)
-        routed_interleave(1, nc.vector.tensor_copy)
+        routed_interleave(2, 4, nc.vector.tensor_copy)
         shared_first(0)
         routed_gate(0, 2, 1)
         routed_gate(0, 2, 0)
@@ -287,16 +295,16 @@ def tile_moe_shf_mlp_gelu_kernel(
         scatter(0, 2, 1)
         routed_turn(4)
         routed_turn(5)
-        routed_interleave(2, nc.scalar.copy)
+        routed_interleave(4, 6, nc.scalar.copy)
         shared_first(1)
         routed_gate(2, 4, 1)
         routed_quantize(2)
-        routed_second(2, 1)
-        routed_second(2, 0)
         routed_gate(2, 4, 0, 8 * HS)
         scatter(2, 4, 0)
         for tb in range(2, 6):
             shared_first(tb)
+        routed_second(2, 1)
+        routed_second(2, 0)
         routed_gate(4, 6, 1)
         routed_gate(4, 6, 0)
         scatter(2, 4, 1)
@@ -304,9 +312,11 @@ def tile_moe_shf_mlp_gelu_kernel(
         shared_second(0)
         scatter(4, 6, 0)
         scatter(4, 6, 1)
-        for c in range(len(CHUNKS)):
-            if c + 1 < len(CHUNKS):
-                shared_quantize(c + 1)
-                shared_second(c + 1)
-            for nb in range(NB):
+        for c in range(1, len(CHUNKS)):
+            shared_quantize(c)
+            shared_second(c)
+        for nb in range(NB):
+            for c in range(len(CHUNKS) - 1):
                 finish(nb, c)
+        for nb in range(NB):
+            finish(nb, len(CHUNKS) - 1)

@@ -25,13 +25,14 @@ NB = N // P
 PAIRS = E // 2
 CHUNKS = ((0, 256), (256, 512), (512, 768))
 W1_GROUPS = ((0, 2), (2, 4), (4, 6))
+W2_GROUPS = ((0, 2), (2, 6))
 WORD_GROUPS = ((0, 1), (1, 2), (2, 4), (4, 6))
 SCALE_GROUPS = ((0, 1), (1, 4), (4, 6))
-ROUTED_PRE = ((0, 5), (1, 6), (2,), (5,), (6,), (2,))
-TURNED = (3, 4, 0, 0, 4, 4)
-ROUTED_Y = ((3, 4), (5, 6), (0, 1))
-SHARED_PRE = (7, 3, 4, 6, 3, 5)
-SHARED_Y = (2, 7, 4)
+ROUTED_PRE = ((0, 5), (1, 6), (2, 4), (3,), (2,), (4,))
+TURNED = (6, 6, 3, 3, 5, 5)
+ROUTED_Y = ((0, 5), (1, 6), (3, 4))
+SHARED_PRE = (7, 0, 5, 6, 0, 1)
+SHARED_Y = (2, 7, 5)
 
 
 def tile_moe_shf_mlp_gelu_kernel(
@@ -50,7 +51,7 @@ def tile_moe_shf_mlp_gelu_kernel(
         xs = keep.tile([P, T], U8, name="xs", align_bytes=64)
         w1w = [keep.tile([P, b - a, 2 * H], U8, name="w1w%d" % a, align_bytes=64) for a, b in W1_GROUPS]
         w1sc = keep.tile([P, E, H], U8, name="w1sc", align_bytes=64)
-        w2w = keep.tile([P, E, 2 * N], U8, name="w2w", align_bytes=64)
+        w2w = [keep.tile([P, b - a, 2 * N], U8, name="w2w%d" % a, align_bytes=64) for a, b in W2_GROUPS]
         w2sc = keep.tile([P, E, N], U8, name="w2sc", align_bytes=64)
         v1w = keep.tile([P, HS], I32, name="v1w", align_bytes=64)
         v1sc = reuse.tile([P, HS], U8, name="v1sc", align_bytes=64, offset=0)
@@ -92,15 +93,15 @@ def tile_moe_shf_mlp_gelu_kernel(
         for r in range(4):
             load_expert_planes(w1sc, w1_scales, r)
         load_words(w1w[1], w1_words, *W1_GROUPS[1])
-        nc.sync.dma_start(out=v1w[:], in_=w1s_words[0].rearrange("p l d -> p (l d)").bitcast(I32))
-        load_plane(v1sc, w1s_scales, 1)
         load_words(w1w[2], w1_words, *W1_GROUPS[2])
-        for r in range(2, 4):
+        nc.sync.dma_start(out=v1w[:], in_=w1s_words[0].rearrange("p l d -> p (l d)").bitcast(I32))
+        for r in range(1, 4):
             load_plane(v1sc, w1s_scales, r)
-        load_words(w2w, w2_words, 0, E)
+        load_words(w2w[0], w2_words, *W2_GROUPS[0])
+        nc.sync.dma_start(out=g_first[:], in_=gate[:, : 2 * C])
         for r in range(4):
             load_expert_planes(w2sc, w2_scales, r)
-        nc.sync.dma_start(out=g_first[:], in_=gate[:, : 2 * C])
+        load_words(w2w[1], w2_words, *W2_GROUPS[1])
         nc.sync.dma_start(out=g_rest[:], in_=gate[:, 2 * C :])
         nc.sync.dma_start(out=v2w[:], in_=w2s_words[0].rearrange("p n d -> p (n d)").bitcast(I32))
         for r in range(4):
@@ -130,7 +131,7 @@ def tile_moe_shf_mlp_gelu_kernel(
             w = w1w[e // 2][:, e % 2, :]
             pre = [bank[i] for i in ROUTED_PRE[e]]
             h_rows[e] = keep.tile([P, H], BF16, name="h_rows%d" % e, align_bytes=64)
-            parts = 2 if e < 2 else 1
+            parts = len(ROUTED_PRE[e])
             width = H // parts
             for a in range(0, H, width):
                 nc.tensor.matmul_mx(
@@ -148,10 +149,6 @@ def tile_moe_shf_mlp_gelu_kernel(
             pairs = h_rows[e][:].bitcast(F32)
             for u in range(2):
                 nc.tensor.transpose(turned(e)[:, e % 2, u, :], pairs[:, u * P : (u + 1) * P], ident[:])
-
-        def routed_first(e):
-            routed_activate(e)
-            routed_turn(e)
 
         h_in, h_codes, gated = {}, {}, {}
 
@@ -184,7 +181,7 @@ def tile_moe_shf_mlp_gelu_kernel(
                 e = 2 * pair + i
                 nc.tensor.matmul_mx(
                     out=bank[ROUTED_Y[pair][nb]][:, i * C : (i + 1) * C],
-                    lhsT=w2w[:, e, 2 * nb * P : 2 * (nb + 1) * P].bitcast(FP4X4),
+                    lhsT=w2w[min(pair, 1)][:, e - 2 * min(pair, 1), 2 * nb * P : 2 * (nb + 1) * P].bitcast(FP4X4),
                     lhsT_scale=w2sc[:, e, nb * P : (nb + 1) * P],
                     rhs=codes[:, i * C : (i + 1) * C].bitcast(FP8X4), rhs_scale=scales[:, i * C : (i + 1) * C],
                     start=True, stop=True,
@@ -274,10 +271,12 @@ def tile_moe_shf_mlp_gelu_kernel(
             gather_words(a, b)
         v1w_perm = permute(v1w, I32, 4)
         for e in range(4):
-            routed_first(e)
+            routed_activate(e)
+            if e % 2:
+                routed_turn(e - 1)
+                routed_turn(e)
         gather_scales(*SCALE_GROUPS[2])
-        routed_interleave(0, 1, nc.vector.tensor_copy)
-        routed_interleave(1, 2, nc.vector.tensor_copy)
+        routed_interleave(0, 2, nc.vector.tensor_copy)
         v1sc_perm = permute(v1sc, U8, 16)
         routed_quantize(0)
         routed_second(0, 1)

@@ -54,7 +54,7 @@ def tile_moe_shf_mlp_gelu_kernel(
         w2w = [keep.tile([P, b - a, 2 * N], U8, name="w2w%d" % a, align_bytes=64) for a, b in W2_GROUPS]
         w2sc = keep.tile([P, E, N], U8, name="w2sc", align_bytes=64)
         v1w = keep.tile([P, HS], I32, name="v1w", align_bytes=64)
-        v1sc = reuse.tile([P, HS], U8, name="v1sc", align_bytes=64, offset=0)
+        v1sc = keep.tile([P, HS], U8, name="v1sc", align_bytes=64)
         v2w = keep.tile([P, N], I32, name="v2w", align_bytes=64)
         v2sc = keep.tile([P, N], U8, name="v2sc", align_bytes=64)
         g_first = reuse.tile([P, 2 * C], F32, name="g_first", align_bytes=64, offset=4 * HS)
@@ -168,10 +168,7 @@ def tile_moe_shf_mlp_gelu_kernel(
                 codes = reuse.tile([P, 2 * C], U32, name="h_codes1", align_bytes=64, offset=4 * HS)
             else:
                 codes = keep.tile([P, 2 * C], U32, name="h_codes%d" % pair, align_bytes=64)
-            if pair == 0:
-                scales = reuse.tile([P, 2 * C], U8, name="h_scales0", align_bytes=64, offset=0)
-            else:
-                scales = keep.tile([P, 2 * C], U8, name="h_scales%d" % pair, align_bytes=64)
+            scales = keep.tile([P, 2 * C], U8, name="h_scales%d" % pair, align_bytes=64)
             nc.vector.quantize_mx(out=codes[:].bitcast(FP8X4), scales=scales[:], in_=h_in[pair][:])
             h_codes[pair] = (codes, scales)
 
@@ -198,12 +195,13 @@ def tile_moe_shf_mlp_gelu_kernel(
                 out=gated[a, nb][:], in0=bank[ROUTED_Y[a // 2][nb]][:, cols], in1=g[a // 2][:, cols], op=MULT
             )
 
-        def scatter(a, b, nb):
+        def scatter(a, b, nb, on_vector):
             places = win[nb][:].indirect(offsets[:, a * C // 16 : b * C // 16])
-            if nb == 0:
-                nc.vector.tensor_copy(out=places, in_=gated[a, nb][:])
+            values = gated[a - a % 2, nb][:, a % 2 * C : (a % 2 + b - a) * C]
+            if on_vector:
+                nc.vector.tensor_copy(out=places, in_=values)
             else:
-                nc.scalar.activation(out=places, in_=gated[a, nb][:], func=COPY)
+                nc.scalar.activation(out=places, in_=values, func=COPY)
 
         ys = {(c, nb): bank[SHARED_Y[c]][:, nb * 256 : (nb + 1) * 256] for c in range(3) for nb in range(NB)}
         hs_in = [keep.tile([P, (b - a) * PACK], BF16, name="hs_in%d" % a, align_bytes=64) for a, b in CHUNKS[:2]]
@@ -211,7 +209,7 @@ def tile_moe_shf_mlp_gelu_kernel(
 
         def permute(src, dtype, run):
             dest = keep.tile([P, HS], dtype, name="perm%d" % run, align_bytes=64)
-            nc.vector.tensor_copy(
+            nc.gpsimd.tensor_copy(
                 out=dest[:].rearrange("p (d a b) -> p a d b", d=PACK, b=run),
                 in_=src[:].rearrange("p (a b d) -> p a d b", d=PACK, b=run),
             )
@@ -290,8 +288,8 @@ def tile_moe_shf_mlp_gelu_kernel(
         routed_quantize(1)
         routed_second(1, 1)
         routed_second(1, 0)
-        scatter(0, 2, 0)
-        scatter(0, 2, 1)
+        scatter(0, 2, 0, True)
+        scatter(0, 2, 1, False)
         routed_turn(4)
         routed_turn(5)
         routed_interleave(4, 6, nc.scalar.copy)
@@ -299,18 +297,18 @@ def tile_moe_shf_mlp_gelu_kernel(
         routed_gate(2, 4, 1)
         routed_quantize(2)
         routed_gate(2, 4, 0, 8 * HS)
-        scatter(2, 4, 0)
+        scatter(2, 4, 0, True)
         for tb in range(2, 6):
             shared_first(tb)
         routed_second(2, 1)
         routed_second(2, 0)
         routed_gate(4, 6, 1)
         routed_gate(4, 6, 0)
-        scatter(2, 4, 1)
+        scatter(2, 4, 1, False)
         shared_quantize(0)
         shared_second(0)
-        scatter(4, 6, 0)
-        scatter(4, 6, 1)
+        scatter(4, 6, 0, True)
+        scatter(4, 6, 1, False)
         for c in range(1, len(CHUNKS)):
             shared_quantize(c)
             shared_second(c)

@@ -24,15 +24,15 @@ PACK = 4
 NB = N // P
 PAIRS = E // 2
 CHUNKS = ((0, 256), (256, 512), (512, 768))
-W1_GROUPS = ((0, 2), (2, 4), (4, 6))
+W1_GROUPS = ((0, 1), (1, 3), (3, 6))
 W2_GROUPS = ((0, 2), (2, 6))
 WORD_GROUPS = ((0, 1), (1, 2), (2, 4), (4, 6))
 SCALE_GROUPS = ((0, 1), (1, 4), (4, 6))
 ROUTED_PRE = ((0, 5), (1, 6), (2, 4), (3,), (2,), (4,))
 TURNED = (6, 6, 3, 3, 5, 5)
-ROUTED_Y = ((0, 5), (1, 6), (3, 4))
-SHARED_PRE = (7, 0, 5, 6, 0, 1)
-SHARED_Y = (2, 7, 5)
+ROUTED_Y = ((0, 5), (5, 6), (3, 4))
+SHARED_PRE = (7, 0, 6, 0, 5, 6)
+SHARED_Y = (2, 7, 1)
 
 
 def tile_moe_shf_mlp_gelu_kernel(
@@ -51,13 +51,16 @@ def tile_moe_shf_mlp_gelu_kernel(
         xs = keep.tile([P, T], U8, name="xs", align_bytes=64)
         w1w = [keep.tile([P, b - a, 2 * H], U8, name="w1w%d" % a, align_bytes=64) for a, b in W1_GROUPS]
         w1sc = keep.tile([P, E, H], U8, name="w1sc", align_bytes=64)
-        w2w = [keep.tile([P, b - a, 2 * N], U8, name="w2w%d" % a, align_bytes=64) for a, b in W2_GROUPS]
+        w2w = [
+            reuse.tile([P, 2, 2 * N], U8, name="w2w0", align_bytes=64, offset=4 * HS),
+            keep.tile([P, E - 2, 2 * N], U8, name="w2w2", align_bytes=64),
+        ]
         w2sc = keep.tile([P, E, N], U8, name="w2sc", align_bytes=64)
         v1w = keep.tile([P, HS], I32, name="v1w", align_bytes=64)
         v1sc = keep.tile([P, HS], U8, name="v1sc", align_bytes=64)
         v2w = keep.tile([P, N], I32, name="v2w", align_bytes=64)
         v2sc = keep.tile([P, N], U8, name="v2sc", align_bytes=64)
-        g_first = reuse.tile([P, 2 * C], F32, name="g_first", align_bytes=64, offset=4 * HS)
+        g_first = keep.tile([P, 2 * C], F32, name="g_first")
         g_rest = keep.tile([P, 4 * C], F32, name="g_rest")
         g = [g_first[:], g_rest[:, : 2 * C], g_rest[:, 2 * C :]]
         ident = keep.tile([P, P], F32, name="ident")
@@ -89,13 +92,12 @@ def tile_moe_shf_mlp_gelu_kernel(
             load_full_plane(nc.sync if q % 2 else nc.scalar, xs, x_scales, q)
         nc.sync.dma_start(out=xw[:].bitcast(I32), in_=x_words[0].rearrange("p t d -> p (t d)").bitcast(I32))
         load_words(w1w[0], w1_words, *W1_GROUPS[0])
-        load_plane(v1sc, w1s_scales, 0)
         for r in range(4):
             load_expert_planes(w1sc, w1_scales, r)
         load_words(w1w[1], w1_words, *W1_GROUPS[1])
         load_words(w1w[2], w1_words, *W1_GROUPS[2])
         nc.sync.dma_start(out=v1w[:], in_=w1s_words[0].rearrange("p l d -> p (l d)").bitcast(I32))
-        for r in range(1, 4):
+        for r in range(4):
             load_plane(v1sc, w1s_scales, r)
         load_words(w2w[0], w2_words, *W2_GROUPS[0])
         nc.sync.dma_start(out=g_first[:], in_=gate[:, : 2 * C])
@@ -128,7 +130,8 @@ def tile_moe_shf_mlp_gelu_kernel(
         h_rows = {}
 
         def routed_activate(e):
-            w = w1w[e // 2][:, e % 2, :]
+            group = max(i for i, (a, b) in enumerate(W1_GROUPS) if a <= e)
+            w = w1w[group][:, e - W1_GROUPS[group][0], :]
             pre = [bank[i] for i in ROUTED_PRE[e]]
             h_rows[e] = keep.tile([P, H], BF16, name="h_rows%d" % e, align_bytes=64)
             parts = len(ROUTED_PRE[e])
@@ -152,9 +155,8 @@ def tile_moe_shf_mlp_gelu_kernel(
 
         h_in, h_codes, gated = {}, {}, {}
 
-        for pair in range(PAIRS - 1):
+        for pair in range(PAIRS):
             h_in[pair] = keep.tile([P, 2 * C * PACK], BF16, name="h_in%d" % pair, align_bytes=64)
-        h_in[2] = reuse.tile([P, 2 * C * PACK], BF16, name="h_in2", align_bytes=64, offset=8 * HS)
 
         def routed_interleave(a, b, copy):
             part = slice(a % 2, a % 2 + b - a)
@@ -195,9 +197,10 @@ def tile_moe_shf_mlp_gelu_kernel(
                 out=gated[a, nb][:], in0=bank[ROUTED_Y[a // 2][nb]][:, cols], in1=g[a // 2][:, cols], op=MULT
             )
 
-        def scatter(a, b, nb, on_vector):
-            places = win[nb][:].indirect(offsets[:, a * C // 16 : b * C // 16])
-            values = gated[a - a % 2, nb][:, a % 2 * C : (a % 2 + b - a) * C]
+        def scatter(pair, nb, on_vector, a=0, b=2 * C):
+            first = pair * 2 * C
+            places = win[nb][:].indirect(offsets[:, (first + a) // 16 : (first + b) // 16])
+            values = gated[2 * pair, nb][:, a:b]
             if on_vector:
                 nc.vector.tensor_copy(out=places, in_=values)
             else:
@@ -287,28 +290,28 @@ def tile_moe_shf_mlp_gelu_kernel(
         routed_gate(0, 2, 0)
         routed_quantize(1)
         routed_second(1, 1)
-        routed_second(1, 0)
-        scatter(0, 2, 0, True)
-        scatter(0, 2, 1, False)
+        scatter(0, 0, True)
+        scatter(0, 1, False)
         routed_turn(4)
         routed_turn(5)
         routed_interleave(4, 6, nc.scalar.copy)
+        routed_second(1, 0)
         shared_first(1)
         routed_gate(2, 4, 1)
         routed_quantize(2)
-        routed_gate(2, 4, 0, 8 * HS)
-        scatter(2, 4, 0, True)
+        routed_gate(2, 4, 0)
+        scatter(1, 0, True)
         for tb in range(2, 6):
             shared_first(tb)
         routed_second(2, 1)
         routed_second(2, 0)
         routed_gate(4, 6, 1)
         routed_gate(4, 6, 0)
-        scatter(2, 4, 1, False)
+        scatter(1, 1, False)
         shared_quantize(0)
         shared_second(0)
-        scatter(4, 6, 0, True)
-        scatter(4, 6, 1, False)
+        scatter(2, 0, True)
+        scatter(2, 1, False)
         for c in range(1, len(CHUNKS)):
             shared_quantize(c)
             shared_second(c)

@@ -21,18 +21,31 @@ ADD = mybir.AluOpType.add
 
 P = 128
 PACK = 4
+QUADRANT = 32
+ROWS = 4
+LIST_COLUMN = 16
+BANK = 512
 NB = N // P
 PAIRS = E // 2
-CHUNKS = ((0, 256), (256, 512), (512, 768))
-W1_GROUPS = ((0, 1), (1, 3), (3, 6))
-W2_GROUPS = ((0, 2), (2, 6))
-WORD_GROUPS = ((0, 1), (1, 2), (2, 4), (4, 6))
-SCALE_GROUPS = ((0, 1), (1, 4), (4, 6))
+PAIR = 2 * C
+CHUNK = 256
+CHUNKS = T // CHUNK
+WARM_UPS = 2
+
+W1_LOADS = ((0, 1), (1, 2), (2, 4), (4, 6))
+W2_LOADS = ((0, 2), (2, 6))
+WORD_GATHERS = ((0, 1), (1, 2), (2, 4), (4, 6))
+SCALE_GATHERS = ((0, 1), (1, 4), (4, 6))
+
 ROUTED_PRE = ((0, 5), (1, 6), (2, 4), (3,), (2,), (4,))
-TURNED = (6, 6, 3, 3, 5, 5)
+TURNED = (6, 3, 5)
 ROUTED_Y = ((0, 5), (5, 6), (3, 4))
 SHARED_PRE = (7, 0, 6, 0, 5, 6)
 SHARED_Y = (2, 7, 1)
+
+SCALES_AT = (512, 768, 512)
+W2_FIRST_AT = 2048
+HS_LAST_AT = 6144
 
 
 def tile_moe_shf_mlp_gelu_kernel(
@@ -44,15 +57,15 @@ def tile_moe_shf_mlp_gelu_kernel(
         keep = ctx.enter_context(tc.tile_pool(name="keep", bufs=1))
         reuse = ctx.enter_context(tc.tile_pool(name="reuse", bufs=1))
         psum = ctx.enter_context(tc.psum_pool(name="psum", bufs=1))
-        bank = [psum.tile([P, 512], F32, name="bank%d" % i) for i in range(8)]
+        bank = [psum.tile([P, BANK], F32, name="bank%d" % i) for i in range(8)]
 
-        offsets = keep.tile([P, T // 16], U16, name="offsets")
+        offsets = keep.tile([P, T // LIST_COLUMN], U16, name="offsets")
         xw = keep.tile([P, T], U32, name="xw", align_bytes=64)
         xs = keep.tile([P, T], U8, name="xs", align_bytes=64)
-        w1w = [keep.tile([P, b - a, 2 * H], U8, name="w1w%d" % a, align_bytes=64) for a, b in W1_GROUPS]
+        w1w = [keep.tile([P, b - a, 2 * H], U8, name="w1w%d" % a, align_bytes=64) for a, b in W1_LOADS]
         w1sc = keep.tile([P, E, H], U8, name="w1sc", align_bytes=64)
         w2w = [
-            reuse.tile([P, 2, 2 * N], U8, name="w2w0", align_bytes=64, offset=4 * HS),
+            reuse.tile([P, 2, 2 * N], U8, name="w2w0", align_bytes=64, offset=W2_FIRST_AT),
             keep.tile([P, E - 2, 2 * N], U8, name="w2w2", align_bytes=64),
         ]
         w2sc = keep.tile([P, E, N], U8, name="w2sc", align_bytes=64)
@@ -60,85 +73,89 @@ def tile_moe_shf_mlp_gelu_kernel(
         v1sc = keep.tile([P, HS], U8, name="v1sc", align_bytes=64)
         v2w = keep.tile([P, N], I32, name="v2w", align_bytes=64)
         v2sc = keep.tile([P, N], U8, name="v2sc", align_bytes=64)
-        g_first = keep.tile([P, 2 * C], F32, name="g_first")
-        g_rest = keep.tile([P, 4 * C], F32, name="g_rest")
-        g = [g_first[:], g_rest[:, : 2 * C], g_rest[:, 2 * C :]]
+        g_first = keep.tile([P, PAIR], F32, name="g_first")
+        g_rest = keep.tile([P, 2 * PAIR], F32, name="g_rest")
+        g = [g_first[:], g_rest[:, :PAIR], g_rest[:, PAIR:]]
         ident = keep.tile([P, P], F32, name="ident")
         win = [keep.tile([P, T], F32, name="win%d" % nb) for nb in range(NB)]
 
         def load_plane(plane, scales, r):
-            rows = scales[0].bitcast(I32).rearrange("(q r) c -> r q c", r=4)
-            nc.sync.dma_start(out=plane[:].bitcast(I32)[r:P:32], in_=rows[r])
+            rows = scales[0].bitcast(I32).rearrange("(q r) c -> r q c", r=ROWS)
+            nc.sync.dma_start(out=plane[:].bitcast(I32)[r:P:QUADRANT], in_=rows[r])
 
         def load_full_plane(queue, plane, scales, q):
-            rows = scales[0].bitcast(I32).rearrange("(q r) c -> q r c", r=4)
+            rows = scales[0].bitcast(I32).rearrange("(q r) c -> q r c", r=ROWS)
             queue.dma_start(
-                out=plane[:].bitcast(I32)[32 * q : 32 * (q + 1)],
-                in_=rows[q].unsqueeze(0).to_broadcast([8, 4, rows.shape[2]]),
+                out=plane[:].bitcast(I32)[QUADRANT * q : QUADRANT * (q + 1)],
+                in_=rows[q].unsqueeze(0).to_broadcast([QUADRANT // ROWS, ROWS, rows.shape[2]]),
             )
 
         def load_expert_planes(plane, scales, r):
-            rows = scales[:, 0].bitcast(I32).rearrange("e (q r) c -> r q e c", r=4)
-            nc.sync.dma_start(out=plane[:].bitcast(I32)[r:P:32], in_=rows[r])
+            rows = scales[:, 0].bitcast(I32).rearrange("e (q r) c -> r q e c", r=ROWS)
+            nc.sync.dma_start(out=plane[:].bitcast(I32)[r:P:QUADRANT], in_=rows[r])
 
         def load_words(tile, words, a, b):
             nc.sync.dma_start(out=tile[:].bitcast(I32), in_=words[a:b, 0].bitcast(I32).rearrange("e p c -> p e c"))
+
+        def expert_words(tiles, loads, e):
+            i = max(i for i, (a, b) in enumerate(loads) if a <= e)
+            return tiles[i][:, e - loads[i][0], :]
 
         nc.gpsimd.memset(v1sc[:].bitcast(I32), 0)
         make_identity(nc, ident[:])
 
         nc.sync.dma_start(offsets[:], offs)
-        for q in range(4):
+        for q in range(P // QUADRANT):
             load_full_plane(nc.sync if q % 2 else nc.scalar, xs, x_scales, q)
         nc.sync.dma_start(out=xw[:].bitcast(I32), in_=x_words[0].rearrange("p t d -> p (t d)").bitcast(I32))
-        load_words(w1w[0], w1_words, *W1_GROUPS[0])
-        for r in range(4):
+        load_words(w1w[0], w1_words, *W1_LOADS[0])
+        for r in range(ROWS):
             load_expert_planes(w1sc, w1_scales, r)
-        load_words(w1w[1], w1_words, *W1_GROUPS[1])
-        load_words(w1w[2], w1_words, *W1_GROUPS[2])
-        nc.sync.dma_start(out=v1w[:], in_=w1s_words[0].rearrange("p l d -> p (l d)").bitcast(I32))
-        for r in range(4):
+        for i in range(1, len(W1_LOADS)):
+            load_words(w1w[i], w1_words, *W1_LOADS[i])
+        for r in range(ROWS - 1):
             load_plane(v1sc, w1s_scales, r)
-        load_words(w2w[0], w2_words, *W2_GROUPS[0])
-        nc.sync.dma_start(out=g_first[:], in_=gate[:, : 2 * C])
-        for r in range(4):
+        nc.sync.dma_start(out=v1w[:], in_=w1s_words[0].rearrange("p l d -> p (l d)").bitcast(I32))
+        load_plane(v1sc, w1s_scales, ROWS - 1)
+        load_words(w2w[0], w2_words, *W2_LOADS[0])
+        nc.sync.dma_start(out=g_first[:], in_=gate[:, :PAIR])
+        for r in range(ROWS):
             load_expert_planes(w2sc, w2_scales, r)
-        load_words(w2w[1], w2_words, *W2_GROUPS[1])
-        nc.sync.dma_start(out=g_rest[:], in_=gate[:, 2 * C :])
+        load_words(w2w[1], w2_words, *W2_LOADS[1])
+        nc.sync.dma_start(out=g_rest[:], in_=gate[:, PAIR:])
         nc.sync.dma_start(out=v2w[:], in_=w2s_words[0].rearrange("p n d -> p (n d)").bitcast(I32))
-        for r in range(4):
+        for r in range(ROWS):
             load_plane(v2sc, w2s_scales, r)
+
+        def slots(a, b):
+            return offsets[:, a * C // LIST_COLUMN : b * C // LIST_COLUMN]
 
         slot_words, slot_scales = {}, {}
 
         def gather_words(a, b):
             words = keep.tile([P, (b - a) * C], U32, name="xgw%d" % a, align_bytes=64)
-            nc.vector.tensor_copy(out=words[:], in_=xw[:].indirect(offsets[:, a * C // 16 : b * C // 16]))
+            nc.vector.tensor_copy(out=words[:], in_=xw[:].indirect(slots(a, b)))
             for e in range(a, b):
                 slot_words[e] = words[:, (e - a) * C : (e - a + 1) * C]
 
-        def gather_scales(a, b):
-            place = HS + 2 * C if a == 1 else HS
-            scales = reuse.tile([P, (b - a) * C], U8, name="xgs%d" % a, align_bytes=64, offset=place)
-            nc.vector.tensor_copy(out=scales[:], in_=xs[:].indirect(offsets[:, a * C // 16 : b * C // 16]))
+        def gather_scales(i):
+            a, b = SCALE_GATHERS[i]
+            scales = reuse.tile([P, (b - a) * C], U8, name="xgs%d" % a, align_bytes=64, offset=SCALES_AT[i])
+            nc.vector.tensor_copy(out=scales[:], in_=xs[:].indirect(slots(a, b)))
             for e in range(a, b):
                 slot_scales[e] = scales[:, (e - a) * C : (e - a + 1) * C]
-
-        def turned(e):
-            return bank[TURNED[e]][:].rearrange("p (e u s) -> p e u s", e=2, u=2)
 
         h_rows = {}
 
         def routed_activate(e):
-            group = max(i for i, (a, b) in enumerate(W1_GROUPS) if a <= e)
-            w = w1w[group][:, e - W1_GROUPS[group][0], :]
+            w = expert_words(w1w, W1_LOADS, e)
             pre = [bank[i] for i in ROUTED_PRE[e]]
             h_rows[e] = keep.tile([P, H], BF16, name="h_rows%d" % e, align_bytes=64)
-            parts = len(ROUTED_PRE[e])
-            width = H // parts
+            width = H // len(pre)
             for a in range(0, H, width):
                 nc.tensor.matmul_mx(
-                    out=pre[a // width][:, a : a + width], lhsT=slot_words[e].bitcast(FP8X4), lhsT_scale=slot_scales[e],
+                    out=pre[a // width][:, a : a + width],
+                    lhsT=slot_words[e].bitcast(FP8X4), lhsT_scale=slot_scales[e],
                     rhs=w[:, 2 * a : 2 * (a + width)].bitcast(FP4X4), rhs_scale=w1sc[:, e, a : a + width],
                     start=True, stop=True,
                 )
@@ -148,29 +165,30 @@ def tile_moe_shf_mlp_gelu_kernel(
                     in_=pre[a // width][:, a : a + width].rearrange("s (p u v) -> s u p v", u=2, v=2), func=GELU,
                 )
 
-        def routed_turn(e):
-            pairs = h_rows[e][:].bitcast(F32)
-            for u in range(2):
-                nc.tensor.transpose(turned(e)[:, e % 2, u, :], pairs[:, u * P : (u + 1) * P], ident[:])
+        def turned(pair):
+            return bank[TURNED[pair]][:].rearrange("p (e u s) -> p e u s", e=2, u=2)
 
-        h_in, h_codes, gated = {}, {}, {}
+        def routed_turn(pair):
+            for i in range(2):
+                words = h_rows[2 * pair + i][:].bitcast(F32)
+                for u in range(2):
+                    nc.tensor.transpose(turned(pair)[:, i, u, :], words[:, u * P : (u + 1) * P], ident[:])
 
-        for pair in range(PAIRS):
-            h_in[pair] = keep.tile([P, 2 * C * PACK], BF16, name="h_in%d" % pair, align_bytes=64)
+        h_in = [keep.tile([P, PAIR * PACK], BF16, name="h_in%d" % pair, align_bytes=64) for pair in range(PAIRS)]
+        h_codes, gated = {}, {}
 
-        def routed_interleave(a, b, copy):
-            part = slice(a % 2, a % 2 + b - a)
+        def routed_interleave(pair, copy):
             copy(
-                out=h_in[a // 2][:].bitcast(F32).rearrange("p (e s u) -> p e s u", e=2, u=2)[:, part],
-                in_=turned(a).rearrange("p e u s -> p e s u")[:, part],
+                out=h_in[pair][:].bitcast(F32).rearrange("p (e s u) -> p e s u", e=2, u=2),
+                in_=turned(pair).rearrange("p e u s -> p e s u"),
             )
 
         def routed_quantize(pair):
             if pair == 1:
-                codes = reuse.tile([P, 2 * C], U32, name="h_codes1", align_bytes=64, offset=4 * HS)
+                codes = reuse.tile([P, PAIR], U32, name="h_codes1", align_bytes=64, offset=W2_FIRST_AT)
             else:
-                codes = keep.tile([P, 2 * C], U32, name="h_codes%d" % pair, align_bytes=64)
-            scales = keep.tile([P, 2 * C], U8, name="h_scales%d" % pair, align_bytes=64)
+                codes = keep.tile([P, PAIR], U32, name="h_codes%d" % pair, align_bytes=64)
+            scales = keep.tile([P, PAIR], U8, name="h_scales%d" % pair, align_bytes=64)
             nc.vector.quantize_mx(out=codes[:].bitcast(FP8X4), scales=scales[:], in_=h_in[pair][:])
             h_codes[pair] = (codes, scales)
 
@@ -178,37 +196,32 @@ def tile_moe_shf_mlp_gelu_kernel(
             codes, scales = h_codes[pair]
             for i in range(2):
                 e = 2 * pair + i
+                cols = slice(i * C, (i + 1) * C)
                 nc.tensor.matmul_mx(
-                    out=bank[ROUTED_Y[pair][nb]][:, i * C : (i + 1) * C],
-                    lhsT=w2w[min(pair, 1)][:, e - 2 * min(pair, 1), 2 * nb * P : 2 * (nb + 1) * P].bitcast(FP4X4),
+                    out=bank[ROUTED_Y[pair][nb]][:, cols],
+                    lhsT=expert_words(w2w, W2_LOADS, e)[:, 2 * nb * P : 2 * (nb + 1) * P].bitcast(FP4X4),
                     lhsT_scale=w2sc[:, e, nb * P : (nb + 1) * P],
-                    rhs=codes[:, i * C : (i + 1) * C].bitcast(FP8X4), rhs_scale=scales[:, i * C : (i + 1) * C],
-                    start=True, stop=True,
+                    rhs=codes[:, cols].bitcast(FP8X4), rhs_scale=scales[:, cols], start=True, stop=True,
                 )
 
-        def routed_gate(a, b, nb, place=None):
-            name = "gated%d_%d" % (a, nb)
-            if place is None:
-                gated[a, nb] = keep.tile([P, (b - a) * C], F32, name=name)
-            else:
-                gated[a, nb] = reuse.tile([P, (b - a) * C], F32, name=name, align_bytes=64, offset=place)
-            cols = slice(a % 2 * C, (a % 2 + b - a) * C)
+        def routed_gate(pair, nb):
+            gated[pair, nb] = keep.tile([P, PAIR], F32, name="gated%d_%d" % (2 * pair, nb))
             nc.vector.tensor_tensor(
-                out=gated[a, nb][:], in0=bank[ROUTED_Y[a // 2][nb]][:, cols], in1=g[a // 2][:, cols], op=MULT
+                out=gated[pair, nb][:], in0=bank[ROUTED_Y[pair][nb]][:, :PAIR], in1=g[pair], op=MULT
             )
 
-        def scatter(pair, nb, on_vector, a=0, b=2 * C):
-            first = pair * 2 * C
-            places = win[nb][:].indirect(offsets[:, (first + a) // 16 : (first + b) // 16])
-            values = gated[2 * pair, nb][:, a:b]
-            if on_vector:
-                nc.vector.tensor_copy(out=places, in_=values)
+        def scatter(pair, nb):
+            places = win[nb][:].indirect(slots(2 * pair, 2 * pair + 2))
+            if nb == 0:
+                nc.vector.tensor_copy(out=places, in_=gated[pair, nb][:])
             else:
-                nc.scalar.activation(out=places, in_=values, func=COPY)
+                nc.scalar.activation(out=places, in_=gated[pair, nb][:], func=COPY)
 
-        ys = {(c, nb): bank[SHARED_Y[c]][:, nb * 256 : (nb + 1) * 256] for c in range(3) for nb in range(NB)}
-        hs_in = [keep.tile([P, (b - a) * PACK], BF16, name="hs_in%d" % a, align_bytes=64) for a, b in CHUNKS[:2]]
-        hs_in.append(reuse.tile([P, 256 * PACK], BF16, name="hs_in_last", align_bytes=64, offset=12 * HS))
+        ys = {(c, nb): bank[SHARED_Y[c]][:, nb * CHUNK : (nb + 1) * CHUNK] for c in range(CHUNKS) for nb in range(NB)}
+        hs_in = [
+            keep.tile([P, CHUNK * PACK], BF16, name="hs_in%d" % (c * CHUNK), align_bytes=64) for c in range(CHUNKS - 1)
+        ]
+        hs_in.append(reuse.tile([P, CHUNK * PACK], BF16, name="hs_in_last", align_bytes=64, offset=HS_LAST_AT))
 
         def permute(src, dtype, run):
             dest = keep.tile([P, HS], dtype, name="perm%d" % run, align_bytes=64)
@@ -218,33 +231,25 @@ def tile_moe_shf_mlp_gelu_kernel(
             )
             return dest
 
-        def shared_first(tb):
-            pre = bank[SHARED_PRE[tb]][:].rearrange("p (d t) -> p d t", d=PACK)
-            cols = slice(tb * P, (tb + 1) * P)
+        def shared_activate(batch):
+            pre = bank[SHARED_PRE[batch]][:].rearrange("p (d t) -> p d t", d=PACK)
+            cols = slice(batch * P, (batch + 1) * P)
             for d in range(PACK):
                 nc.tensor.matmul_mx(
                     out=pre[:, d, :], lhsT=v1w_perm[:, d * P : (d + 1) * P].bitcast(FP8X4),
                     lhsT_scale=v1sc_perm[:, d * P : (d + 1) * P],
                     rhs=xw[:, cols].bitcast(FP8X4), rhs_scale=xs[:, cols], start=True, stop=True,
                 )
-            c = tb * P // CHUNKS[1][0]
-            place = tb * P - CHUNKS[c][0]
+            c, place = divmod(batch * P, CHUNK)
             nc.scalar.activation(
                 out=hs_in[c][:, place * PACK : (place + P) * PACK].rearrange("p (t d) -> p t d", d=PACK),
                 in_=pre.rearrange("p d t -> p t d"), func=GELU,
             )
 
-        hs_codes = {}
-
-        def shared_quantize(c):
-            width = CHUNKS[c][1] - CHUNKS[c][0]
-            codes = keep.tile([P, width], U32, name="hs_codes%d" % c, align_bytes=64)
-            scales = keep.tile([P, width], U8, name="hs_scales%d" % c, align_bytes=64)
-            nc.vector.quantize_mx(out=codes[:].bitcast(FP8X4), scales=scales[:], in_=hs_in[c][:])
-            hs_codes[c] = (codes, scales)
-
         def shared_second(c):
-            codes, scales = hs_codes[c]
+            codes = keep.tile([P, CHUNK], U32, name="hs_codes%d" % c, align_bytes=64)
+            scales = keep.tile([P, CHUNK], U8, name="hs_scales%d" % c, align_bytes=64)
+            nc.vector.quantize_mx(out=codes[:].bitcast(FP8X4), scales=scales[:], in_=hs_in[c][:])
             for nb in range(NB):
                 nc.tensor.matmul_mx(
                     out=ys[c, nb], lhsT=v2w[:, nb * P : (nb + 1) * P].bitcast(FP8X4),
@@ -253,70 +258,71 @@ def tile_moe_shf_mlp_gelu_kernel(
                 )
 
         def finish(nb, c):
-            cols = slice(*CHUNKS[c])
-            if nb == 0 and c < 2:
-                res = reuse.tile([P, 256], F32, name="res0_%d" % c, align_bytes=64, offset=(12 + 2 * c) * HS)
+            cols = slice(c * CHUNK, (c + 1) * CHUNK)
+            if nb == 0 and c < CHUNKS - 1:
+                res = reuse.tile([P, CHUNK], F32, name="res0_%d" % c, align_bytes=64, offset=HS_LAST_AT + 4 * CHUNK * c)
             else:
-                res = keep.tile([P, cols.stop - cols.start], F32, name="res%d_%d" % (nb, c))
+                res = keep.tile([P, CHUNK], F32, name="res%d_%d" % (nb, c))
             nc.vector.tensor_tensor(out=res[:], in0=ys[c, nb], in1=win[nb][:, cols], op=ADD)
             nc.sync.dma_start(out=out[nb * P : (nb + 1) * P, cols], in_=res[:])
 
-        for i in range(2):
+        for i in range(WARM_UPS):
             nc.tensor.matmul_mx(
-                out=bank[7][:], lhsT=xw[:, :P].bitcast(FP8X4), lhsT_scale=xs[:, :P],
-                rhs=xw[:, :512].bitcast(FP8X4), rhs_scale=xs[:, :512], start=True, stop=True,
+                out=bank[SHARED_PRE[0]][:], lhsT=xw[:, :P].bitcast(FP8X4), lhsT_scale=xs[:, :P],
+                rhs=xw[:, :BANK].bitcast(FP8X4), rhs_scale=xs[:, :BANK], start=True, stop=True,
             )
-        gather_scales(*SCALE_GROUPS[0])
-        gather_scales(*SCALE_GROUPS[1])
-        for a, b in WORD_GROUPS:
+
+        gather_scales(0)
+        gather_scales(1)
+        for a, b in WORD_GATHERS:
             gather_words(a, b)
         v1w_perm = permute(v1w, I32, 4)
-        for e in range(4):
-            routed_activate(e)
-            if e % 2:
-                routed_turn(e - 1)
-                routed_turn(e)
-        gather_scales(*SCALE_GROUPS[2])
-        routed_interleave(0, 2, nc.vector.tensor_copy)
+        for pair in range(2):
+            routed_activate(2 * pair)
+            routed_activate(2 * pair + 1)
+            routed_turn(pair)
+        gather_scales(2)
+        routed_interleave(0, nc.vector.tensor_copy)
         v1sc_perm = permute(v1sc, U8, 16)
+
         routed_quantize(0)
         routed_second(0, 1)
         routed_second(0, 0)
         routed_activate(4)
         routed_activate(5)
-        routed_interleave(2, 4, nc.vector.tensor_copy)
-        shared_first(0)
-        routed_gate(0, 2, 1)
-        routed_gate(0, 2, 0)
+        routed_interleave(1, nc.vector.tensor_copy)
+        shared_activate(0)
+        routed_gate(0, 1)
+        routed_gate(0, 0)
         routed_quantize(1)
         routed_second(1, 1)
-        scatter(0, 0, True)
-        scatter(0, 1, False)
-        routed_turn(4)
-        routed_turn(5)
-        routed_interleave(4, 6, nc.scalar.copy)
+        scatter(0, 0)
+        scatter(0, 1)
+
+        routed_turn(2)
+        routed_interleave(2, nc.scalar.copy)
         routed_second(1, 0)
-        shared_first(1)
-        routed_gate(2, 4, 1)
+        shared_activate(1)
+        routed_gate(1, 1)
         routed_quantize(2)
-        routed_gate(2, 4, 0)
-        scatter(1, 0, True)
-        for tb in range(2, 6):
-            shared_first(tb)
+        routed_gate(1, 0)
+        scatter(1, 0)
+
+        for batch in range(2, T // P):
+            shared_activate(batch)
         routed_second(2, 1)
         routed_second(2, 0)
-        routed_gate(4, 6, 1)
-        routed_gate(4, 6, 0)
-        scatter(1, 1, False)
-        shared_quantize(0)
+        routed_gate(2, 1)
+        routed_gate(2, 0)
+        scatter(1, 1)
         shared_second(0)
-        scatter(2, 0, True)
-        scatter(2, 1, False)
-        for c in range(1, len(CHUNKS)):
-            shared_quantize(c)
+        scatter(2, 0)
+        scatter(2, 1)
+        for c in range(1, CHUNKS):
             shared_second(c)
+
         for nb in range(NB):
-            for c in range(len(CHUNKS) - 1):
+            for c in range(CHUNKS - 1):
                 finish(nb, c)
         for nb in range(NB):
-            finish(nb, len(CHUNKS) - 1)
+            finish(nb, CHUNKS - 1)

@@ -30,7 +30,8 @@ PAIRS = E // 2
 PAIR = 2 * C
 CHUNK = 256
 CHUNKS = T // CHUNK
-WARM_UPS = 2
+WARM_UPS = 6
+FIRST_TOKENS = 256
 
 W1_LOADS = ((0, 1), (1, 2), (2, 4), (4, 6))
 W2_LOADS = ((0, 2), (2, 6))
@@ -107,7 +108,9 @@ def tile_moe_shf_mlp_gelu_kernel(
         nc.sync.dma_start(offsets[:], offs)
         for q in range(P // QUADRANT):
             load_full_plane(nc.sync if q % 2 else nc.scalar, xs, x_scales, q)
-        nc.sync.dma_start(out=xw[:].bitcast(I32), in_=x_words[0].rearrange("p t d -> p (t d)").bitcast(I32))
+        token_words = x_words[0].rearrange("p t d -> p (t d)").bitcast(I32)
+        nc.sync.dma_start(out=xw[:, :FIRST_TOKENS].bitcast(I32), in_=token_words[:, :FIRST_TOKENS])
+        nc.sync.dma_start(out=xw[:, FIRST_TOKENS:].bitcast(I32), in_=token_words[:, FIRST_TOKENS:])
         load_words(w1w[0], w1_words, *W1_LOADS[0])
         for r in range(ROWS):
             load_expert_planes(w1sc, w1_scales, r)
@@ -268,8 +271,8 @@ def tile_moe_shf_mlp_gelu_kernel(
 
         for i in range(WARM_UPS):
             nc.tensor.matmul_mx(
-                out=bank[SHARED_PRE[0]][:], lhsT=xw[:, :P].bitcast(FP8X4), lhsT_scale=xs[:, :P],
-                rhs=xw[:, :BANK].bitcast(FP8X4), rhs_scale=xs[:, :BANK], start=True, stop=True,
+                out=bank[SHARED_PRE[0]][:, :FIRST_TOKENS], lhsT=xw[:, :P].bitcast(FP8X4), lhsT_scale=xs[:, :P],
+                rhs=xw[:, :FIRST_TOKENS].bitcast(FP8X4), rhs_scale=xs[:, :FIRST_TOKENS], start=True, stop=True,
             )
 
         gather_scales(0)

@@ -40,8 +40,9 @@ SCALE_GATHERS = ((0, 1), (1, 4), (4, 6))
 
 ROUTED_PRE = ((0, 5), (1, 6), (2, 4), (3,), (2,), (4,))
 TURNED = (6, 3, 5)
-ROUTED_Y = ((0, 5), (5, 6), (3, 4))
-SHARED_PRE = (7, 0, 6, 0, 5, 6)
+ROUTED_Y = ((0, 5), (3, 6), (5, 4))
+SHARED_PRE = (7, 0, 1, 6, 3, 6)
+FIRST_Y = (0, 1)
 SHARED_Y = (2, 7, 1)
 
 SCALES_AT = (512, 768, 512)
@@ -124,8 +125,8 @@ def tile_moe_shf_mlp_gelu_kernel(
         nc.sync.dma_start(out=g_first[:], in_=gate[:, :PAIR])
         for r in range(ROWS):
             load_expert_planes(w2sc, w2_scales, r)
-        load_words(w2w[1], w2_words, *W2_LOADS[1])
         nc.sync.dma_start(out=g_rest[:], in_=gate[:, PAIR:])
+        load_words(w2w[1], w2_words, *W2_LOADS[1])
         nc.sync.dma_start(out=v2w[:], in_=w2s_words[0].rearrange("p n d -> p (n d)").bitcast(I32))
         for r in range(ROWS):
             load_plane(v2sc, w2s_scales, r)
@@ -187,8 +188,8 @@ def tile_moe_shf_mlp_gelu_kernel(
             )
 
         def routed_quantize(pair):
-            if pair == 1:
-                codes = reuse.tile([P, PAIR], U32, name="h_codes1", align_bytes=64, offset=W2_FIRST_AT)
+            if pair > 0:
+                codes = reuse.tile([P, PAIR], U32, name="h_codes%d" % pair, align_bytes=64, offset=W2_FIRST_AT)
             else:
                 codes = keep.tile([P, PAIR], U32, name="h_codes%d" % pair, align_bytes=64)
             scales = keep.tile([P, PAIR], U8, name="h_scales%d" % pair, align_bytes=64)
@@ -201,7 +202,7 @@ def tile_moe_shf_mlp_gelu_kernel(
                 e = 2 * pair + i
                 cols = slice(i * C, (i + 1) * C)
                 nc.tensor.matmul_mx(
-                    out=bank[ROUTED_Y[pair][nb]][:, cols],
+                    out=bank[FIRST_Y[i] if (pair, nb) == (0, 0) else ROUTED_Y[pair][nb]][:, cols],
                     lhsT=expert_words(w2w, W2_LOADS, e)[:, 2 * nb * P : 2 * (nb + 1) * P].bitcast(FP4X4),
                     lhsT_scale=w2sc[:, e, nb * P : (nb + 1) * P],
                     rhs=codes[:, cols].bitcast(FP8X4), rhs_scale=scales[:, cols], start=True, stop=True,
@@ -219,6 +220,16 @@ def tile_moe_shf_mlp_gelu_kernel(
                 nc.vector.tensor_copy(out=places, in_=gated[pair, nb][:])
             else:
                 nc.scalar.activation(out=places, in_=gated[pair, nb][:], func=COPY)
+
+        def copy_out(pair, nb):
+            gated[pair, nb] = keep.tile([P, PAIR], F32, name="plain%d_%d" % (2 * pair, nb))
+            for i in range(2):
+                cols = slice(i * C, (i + 1) * C)
+                nc.scalar.copy(out=gated[pair, nb][:, cols], in_=bank[FIRST_Y[i]][:, cols])
+
+        def scatter_gated(pair):
+            places = win[0][:].indirect(slots(2 * pair, 2 * pair + 2))
+            nc.vector.tensor_tensor(out=places, in0=gated[pair, 0][:], in1=g[pair], op=MULT)
 
         ys = {(c, nb): bank[SHARED_Y[c]][:, nb * CHUNK : (nb + 1) * CHUNK] for c in range(CHUNKS) for nb in range(NB)}
         hs_in = [
@@ -296,36 +307,36 @@ def tile_moe_shf_mlp_gelu_kernel(
         routed_interleave(1, nc.vector.tensor_copy)
         shared_activate(0)
         routed_gate(0, 1)
-        routed_gate(0, 0)
+        copy_out(0, 0)
         routed_quantize(1)
         routed_second(1, 1)
-        scatter(0, 0)
+        routed_second(1, 0)
+        scatter_gated(0)
         scatter(0, 1)
 
         routed_turn(2)
         routed_interleave(2, nc.scalar.copy)
-        routed_second(1, 0)
         shared_activate(1)
         routed_gate(1, 1)
-        routed_quantize(2)
         routed_gate(1, 0)
+        routed_quantize(2)
         scatter(1, 0)
 
-        for batch in range(2, T // P):
-            shared_activate(batch)
+        shared_activate(2)
+        shared_activate(3)
+        scatter(1, 1)
+        shared_activate(4)
+        shared_activate(5)
+        shared_second(0)
+        shared_second(1)
         routed_second(2, 1)
         routed_second(2, 0)
         routed_gate(2, 1)
         routed_gate(2, 0)
-        scatter(1, 1)
-        shared_second(0)
         scatter(2, 0)
         scatter(2, 1)
-        for c in range(1, CHUNKS):
-            shared_second(c)
+        shared_second(2)
 
         for nb in range(NB):
-            for c in range(CHUNKS - 1):
+            for c in range(CHUNKS):
                 finish(nb, c)
-        for nb in range(NB):
-            finish(nb, CHUNKS - 1)

@@ -38,7 +38,7 @@ W2_LOADS = ((0, 2), (2, 6))
 WORD_GATHERS = ((0, 1), (1, 2), (2, 4), (4, 6))
 SCALE_GATHERS = ((0, 1), (1, 4), (4, 6))
 
-ROUTED_PRE = ((0, 5), (1, 6), (2, 4), (3,), (2,), (4,))
+ROUTED_PRE = ((0, 5), (1,), (2, 4), (3,), (2,), (4,))
 TURNED = (6, 3, 5)
 ROUTED_Y = ((0, 5), (3, 6), (5, 4))
 SHARED_PRE = (7, 0, 1, 6, 3, 6)

@@ -40,10 +40,10 @@ SCALE_GATHERS = ((0, 1), (1, 4), (4, 6))
 
 ROUTED_PRE = ((0, 5), (1,), (2, 4), (3,), (2,), (4,))
 TURNED = (6, 3, 5)
-ROUTED_Y = ((0, 5), (3, 6), (5, 4))
-SHARED_PRE = (7, 0, 1, 6, 3, 6)
+ROUTED_Y = ((0, 5), (3, 6), (6, 6))
+SHARED_PRE = (7, 0, 1, 6, 3, 1)
 FIRST_Y = (0, 1)
-SHARED_Y = (2, 7, 1)
+SHARED_Y = ((1, 0), (7, 0)), ((1, 1), (2, 0)), ((4, 0), (5, 0))
 
 SCALES_AT = (512, 768, 512)
 W2_FIRST_AT = 2048
@@ -196,13 +196,17 @@ def tile_moe_shf_mlp_gelu_kernel(
             nc.vector.quantize_mx(out=codes[:].bitcast(FP8X4), scales=scales[:], in_=h_in[pair][:])
             h_codes[pair] = (codes, scales)
 
+        def routed_y(pair, nb):
+            first = PAIR * nb if pair == 2 else 0
+            return bank[ROUTED_Y[pair][nb]][:, first : first + PAIR]
+
         def routed_second(pair, nb):
             codes, scales = h_codes[pair]
             for i in range(2):
                 e = 2 * pair + i
                 cols = slice(i * C, (i + 1) * C)
                 nc.tensor.matmul_mx(
-                    out=bank[FIRST_Y[i] if (pair, nb) == (0, 0) else ROUTED_Y[pair][nb]][:, cols],
+                    out=bank[FIRST_Y[i]][:, cols] if (pair, nb) == (0, 0) else routed_y(pair, nb)[:, cols],
                     lhsT=expert_words(w2w, W2_LOADS, e)[:, 2 * nb * P : 2 * (nb + 1) * P].bitcast(FP4X4),
                     lhsT_scale=w2sc[:, e, nb * P : (nb + 1) * P],
                     rhs=codes[:, cols].bitcast(FP8X4), rhs_scale=scales[:, cols], start=True, stop=True,
@@ -210,9 +214,7 @@ def tile_moe_shf_mlp_gelu_kernel(
 
         def routed_gate(pair, nb):
             gated[pair, nb] = keep.tile([P, PAIR], F32, name="gated%d_%d" % (2 * pair, nb))
-            nc.vector.tensor_tensor(
-                out=gated[pair, nb][:], in0=bank[ROUTED_Y[pair][nb]][:, :PAIR], in1=g[pair], op=MULT
-            )
+            nc.vector.tensor_tensor(out=gated[pair, nb][:], in0=routed_y(pair, nb), in1=g[pair], op=MULT)
 
         def scatter(pair, nb):
             places = win[nb][:].indirect(slots(2 * pair, 2 * pair + 2))
@@ -231,11 +233,11 @@ def tile_moe_shf_mlp_gelu_kernel(
             places = win[0][:].indirect(slots(2 * pair, 2 * pair + 2))
             nc.vector.tensor_tensor(out=places, in0=gated[pair, 0][:], in1=g[pair], op=MULT)
 
-        ys = {(c, nb): bank[SHARED_Y[c]][:, nb * CHUNK : (nb + 1) * CHUNK] for c in range(CHUNKS) for nb in range(NB)}
-        hs_in = [
-            keep.tile([P, CHUNK * PACK], BF16, name="hs_in%d" % (c * CHUNK), align_bytes=64) for c in range(CHUNKS - 1)
-        ]
-        hs_in.append(reuse.tile([P, CHUNK * PACK], BF16, name="hs_in_last", align_bytes=64, offset=HS_LAST_AT))
+        ys = {
+            (c, nb): bank[SHARED_Y[c][nb][0]][:, SHARED_Y[c][nb][1] * CHUNK : (SHARED_Y[c][nb][1] + 1) * CHUNK]
+            for c in range(CHUNKS) for nb in range(NB)
+        }
+        hs_in = [keep.tile([P, CHUNK * PACK], BF16, name="hs_in%d" % c, align_bytes=64) for c in range(CHUNKS)]
 
         def permute(src, dtype, run):
             dest = keep.tile([P, HS], dtype, name="perm%d" % run, align_bytes=64)
@@ -260,23 +262,25 @@ def tile_moe_shf_mlp_gelu_kernel(
                 in_=pre.rearrange("p d t -> p t d"), func=GELU,
             )
 
-        def shared_second(c):
+        hs_codes = {}
+
+        def shared_quantize(c):
             codes = keep.tile([P, CHUNK], U32, name="hs_codes%d" % c, align_bytes=64)
             scales = keep.tile([P, CHUNK], U8, name="hs_scales%d" % c, align_bytes=64)
             nc.vector.quantize_mx(out=codes[:].bitcast(FP8X4), scales=scales[:], in_=hs_in[c][:])
-            for nb in range(NB):
-                nc.tensor.matmul_mx(
-                    out=ys[c, nb], lhsT=v2w[:, nb * P : (nb + 1) * P].bitcast(FP8X4),
-                    lhsT_scale=v2sc[:, nb * P : (nb + 1) * P],
-                    rhs=codes[:].bitcast(FP8X4), rhs_scale=scales[:], start=True, stop=True,
-                )
+            hs_codes[c] = (codes, scales)
+
+        def shared_second(c, nb):
+            codes, scales = hs_codes[c]
+            nc.tensor.matmul_mx(
+                out=ys[c, nb], lhsT=v2w[:, nb * P : (nb + 1) * P].bitcast(FP8X4),
+                lhsT_scale=v2sc[:, nb * P : (nb + 1) * P],
+                rhs=codes[:].bitcast(FP8X4), rhs_scale=scales[:], start=True, stop=True,
+            )
 
         def finish(nb, c):
             cols = slice(c * CHUNK, (c + 1) * CHUNK)
-            if nb == 0 and c < CHUNKS - 1:
-                res = reuse.tile([P, CHUNK], F32, name="res0_%d" % c, align_bytes=64, offset=HS_LAST_AT + 4 * CHUNK * c)
-            else:
-                res = keep.tile([P, CHUNK], F32, name="res%d_%d" % (nb, c))
+            res = keep.tile([P, CHUNK], F32, name="res%d_%d" % (nb, c))
             nc.vector.tensor_tensor(out=res[:], in0=ys[c, nb], in1=win[nb][:, cols], op=ADD)
             nc.sync.dma_start(out=out[nb * P : (nb + 1) * P, cols], in_=res[:])
 
@@ -327,15 +331,20 @@ def tile_moe_shf_mlp_gelu_kernel(
         scatter(1, 1)
         shared_activate(4)
         shared_activate(5)
-        shared_second(0)
-        shared_second(1)
+        for c in range(2):
+            shared_quantize(c)
+            shared_second(c, 1)
         routed_second(2, 1)
         routed_second(2, 0)
-        routed_gate(2, 1)
         routed_gate(2, 0)
+        routed_gate(2, 1)
+        shared_second(0, 0)
+        shared_second(1, 0)
         scatter(2, 0)
         scatter(2, 1)
-        shared_second(2)
+        shared_quantize(2)
+        shared_second(2, 0)
+        shared_second(2, 1)
 
         for nb in range(NB):
             for c in range(CHUNKS):

@@ -38,12 +38,12 @@ W2_LOADS = ((0, 2), (2, 6))
 WORD_GATHERS = ((0, 1), (1, 2), (2, 4), (4, 6))
 SCALE_GATHERS = ((0, 1), (1, 4), (4, 6))
 
-ROUTED_PRE = ((0, 5), (1,), (2, 4), (3,), (2,), (4,))
+ROUTED_PRE = ((0,), (1,), (2,), (3,), (2,), (1,))
 TURNED = (6, 3, 5)
 ROUTED_Y = ((0, 5), (3, 6), (6, 6))
-SHARED_PRE = (7, 0, 1, 6, 3, 1)
-FIRST_Y = (0, 1)
-SHARED_Y = ((1, 0), (7, 0)), ((1, 1), (2, 0)), ((4, 0), (5, 0))
+SHARED_PRE = (7, 0, 4, 6, 3, 4)
+FIRST_Y = (0, 4)
+SHARED_Y = ((4, 0), (7, 0)), ((4, 1), (2, 0)), ((1, 0), (5, 0))
 
 SCALES_AT = (512, 768, 512)
 W2_FIRST_AT = 2048
@@ -117,10 +117,9 @@ def tile_moe_shf_mlp_gelu_kernel(
             load_expert_planes(w1sc, w1_scales, r)
         for i in range(1, len(W1_LOADS)):
             load_words(w1w[i], w1_words, *W1_LOADS[i])
-        for r in range(ROWS - 1):
+        for r in range(ROWS):
             load_plane(v1sc, w1s_scales, r)
         nc.sync.dma_start(out=v1w[:], in_=w1s_words[0].rearrange("p l d -> p (l d)").bitcast(I32))
-        load_plane(v1sc, w1s_scales, ROWS - 1)
         load_words(w2w[0], w2_words, *W2_LOADS[0])
         nc.sync.dma_start(out=g_first[:], in_=gate[:, :PAIR])
         for r in range(ROWS):
@@ -294,6 +293,7 @@ def tile_moe_shf_mlp_gelu_kernel(
         gather_scales(1)
         for a, b in WORD_GATHERS:
             gather_words(a, b)
+        v1sc_perm = permute(v1sc, U8, 16)
         v1w_perm = permute(v1w, I32, 4)
         for pair in range(2):
             routed_activate(2 * pair)
@@ -301,7 +301,6 @@ def tile_moe_shf_mlp_gelu_kernel(
             routed_turn(pair)
         gather_scales(2)
         routed_interleave(0, nc.vector.tensor_copy)
-        v1sc_perm = permute(v1sc, U8, 16)
 
         routed_quantize(0)
         routed_second(0, 1)

@@ -38,7 +38,7 @@ W2_LOADS = ((0, 2), (2, 6))
 WORD_GATHERS = ((0, 1), (1, 2), (2, 4), (4, 6))
 SCALE_GATHERS = ((0, 1), (1, 4), (4, 6))
 
-ROUTED_PRE = ((0,), (1,), (2,), (3,), (2,), (1,))
+ROUTED_PRE = ((0, 5), (1,), (2,), (4,), (2,), (1,))
 TURNED = (6, 3, 5)
 ROUTED_Y = ((0, 5), (3, 6), (6, 6))
 SHARED_PRE = (7, 0, 4, 6, 3, 4)

@@ -30,7 +30,6 @@ PAIRS = E // 2
 PAIR = 2 * C
 CHUNK = 256
 CHUNKS = T // CHUNK
-WARM_UPS = 6
 FIRST_TOKENS = 256
 
 W1_LOADS = ((0, 1), (1, 2), (2, 4), (4, 6))
@@ -282,12 +281,6 @@ def tile_moe_shf_mlp_gelu_kernel(
             res = keep.tile([P, CHUNK], F32, name="res%d_%d" % (nb, c))
             nc.vector.tensor_tensor(out=res[:], in0=ys[c, nb], in1=win[nb][:, cols], op=ADD)
             nc.sync.dma_start(out=out[nb * P : (nb + 1) * P, cols], in_=res[:])
-
-        for i in range(WARM_UPS):
-            nc.tensor.matmul_mx(
-                out=bank[SHARED_PRE[0]][:, :FIRST_TOKENS], lhsT=xw[:, :P].bitcast(FP8X4), lhsT_scale=xs[:, :P],
-                rhs=xw[:, :FIRST_TOKENS].bitcast(FP8X4), rhs_scale=xs[:, :FIRST_TOKENS], start=True, stop=True,
-            )
 
         gather_scales(0)
         gather_scales(1)

from contextlib import ExitStack

import concourse.mybir as mybir
from concourse.masks import make_identity

K, T, E, C, H, HS, N = 512, 768, 6, 128, 512, 512, 256
FLOPS = 2 * T * (K * H + H * N + K * HS + HS * N)

F32 = mybir.dt.float32
BF16 = mybir.dt.bfloat16
I32 = mybir.dt.int32
U32 = mybir.dt.uint32
U16 = mybir.dt.uint16
U8 = mybir.dt.uint8
FP8X4 = mybir.dt.float8_e4m3fn_x4
FP4X4 = mybir.dt.float4_e2m1fn_x4
GELU = mybir.ActivationFunctionType.Gelu_apprx_tanh
COPY = mybir.ActivationFunctionType.Copy
MULT = mybir.AluOpType.mult
ADD = mybir.AluOpType.add

P = 128
PACK = 4
QUADRANT = 32
ROWS = 4
LIST_COLUMN = 16
BANK = 512
NB = N // P
PAIRS = E // 2
PAIR = 2 * C
CHUNK = 256
CHUNKS = T // CHUNK
FIRST_TOKENS = 256

W1_LOADS = ((0, 1), (1, 2), (2, 4), (4, 6))
W2_LOADS = ((0, 2), (2, 6))
WORD_GATHERS = ((0, 1), (1, 2), (2, 4), (4, 6))
SCALE_GATHERS = ((0, 1), (1, 4), (4, 6))

ROUTED_PRE = ((0, 5), (1,), (2,), (4,), (2,), (1,))
TURNED = (6, 3, 5)
ROUTED_Y = ((0, 5), (3, 6), (6, 6))
SHARED_PRE = (7, 0, 4, 6, 3, 4)
FIRST_Y = (0, 4)
SHARED_Y = ((4, 0), (7, 0)), ((4, 1), (2, 0)), ((1, 0), (5, 0))

SCALES_AT = (512, 768, 512)
W2_FIRST_AT = 2048
HS_LAST_AT = 6144


def tile_moe_shf_mlp_gelu_kernel(
    tc, x_words, x_scales, w1_words, w1_scales, w2_words, w2_scales,
    w1s_words, w1s_scales, w2s_words, w2s_scales, gate, offs, out,
):
    nc = tc.nc
    with ExitStack() as ctx:
        keep = ctx.enter_context(tc.tile_pool(name="keep", bufs=1))
        reuse = ctx.enter_context(tc.tile_pool(name="reuse", bufs=1))
        psum = ctx.enter_context(tc.psum_pool(name="psum", bufs=1))
        bank = [psum.tile([P, BANK], F32, name="bank%d" % i) for i in range(8)]

        offsets = keep.tile([P, T // LIST_COLUMN], U16, name="offsets")
        xw = keep.tile([P, T], U32, name="xw", align_bytes=64)
        xs = keep.tile([P, T], U8, name="xs", align_bytes=64)
        w1w = [keep.tile([P, b - a, 2 * H], U8, name="w1w%d" % a, align_bytes=64) for a, b in W1_LOADS]
        w1sc = keep.tile([P, E, H], U8, name="w1sc", align_bytes=64)
        w2w = [
            reuse.tile([P, 2, 2 * N], U8, name="w2w0", align_bytes=64, offset=W2_FIRST_AT),
            keep.tile([P, E - 2, 2 * N], U8, name="w2w2", align_bytes=64),
        ]
        w2sc = keep.tile([P, E, N], U8, name="w2sc", align_bytes=64)
        v1w = keep.tile([P, HS], I32, name="v1w", align_bytes=64)
        v1sc = keep.tile([P, HS], U8, name="v1sc", align_bytes=64)
        v2w = keep.tile([P, N], I32, name="v2w", align_bytes=64)
        v2sc = keep.tile([P, N], U8, name="v2sc", align_bytes=64)
        g_first = keep.tile([P, PAIR], F32, name="g_first")
        g_rest = keep.tile([P, 2 * PAIR], F32, name="g_rest")
        g = [g_first[:], g_rest[:, :PAIR], g_rest[:, PAIR:]]
        ident = keep.tile([P, P], F32, name="ident")
        win = [keep.tile([P, T], F32, name="win%d" % nb) for nb in range(NB)]

        def load_plane(plane, scales, r):
            rows = scales[0].bitcast(I32).rearrange("(q r) c -> r q c", r=ROWS)
            nc.sync.dma_start(out=plane[:].bitcast(I32)[r:P:QUADRANT], in_=rows[r])

        def load_full_plane(queue, plane, scales, q):
            rows = scales[0].bitcast(I32).rearrange("(q r) c -> q r c", r=ROWS)
            queue.dma_start(
                out=plane[:].bitcast(I32)[QUADRANT * q : QUADRANT * (q + 1)],
                in_=rows[q].unsqueeze(0).to_broadcast([QUADRANT // ROWS, ROWS, rows.shape[2]]),
            )

        def load_expert_planes(plane, scales, r):
            rows = scales[:, 0].bitcast(I32).rearrange("e (q r) c -> r q e c", r=ROWS)
            nc.sync.dma_start(out=plane[:].bitcast(I32)[r:P:QUADRANT], in_=rows[r])

        def load_words(tile, words, a, b):
            nc.sync.dma_start(out=tile[:].bitcast(I32), in_=words[a:b, 0].bitcast(I32).rearrange("e p c -> p e c"))

        def expert_words(tiles, loads, e):
            i = max(i for i, (a, b) in enumerate(loads) if a <= e)
            return tiles[i][:, e - loads[i][0], :]

        nc.gpsimd.memset(v1sc[:].bitcast(I32), 0)
        make_identity(nc, ident[:])

        nc.sync.dma_start(offsets[:], offs)
        for q in range(P // QUADRANT):
            load_full_plane(nc.sync if q % 2 else nc.scalar, xs, x_scales, q)
        token_words = x_words[0].rearrange("p t d -> p (t d)").bitcast(I32)
        nc.sync.dma_start(out=xw[:, :FIRST_TOKENS].bitcast(I32), in_=token_words[:, :FIRST_TOKENS])
        nc.sync.dma_start(out=xw[:, FIRST_TOKENS:].bitcast(I32), in_=token_words[:, FIRST_TOKENS:])
        load_words(w1w[0], w1_words, *W1_LOADS[0])
        for r in range(ROWS):
            load_expert_planes(w1sc, w1_scales, r)
        for i in range(1, len(W1_LOADS)):
            load_words(w1w[i], w1_words, *W1_LOADS[i])
        for r in range(ROWS):
            load_plane(v1sc, w1s_scales, r)
        nc.sync.dma_start(out=v1w[:], in_=w1s_words[0].rearrange("p l d -> p (l d)").bitcast(I32))
        load_words(w2w[0], w2_words, *W2_LOADS[0])
        nc.sync.dma_start(out=g_first[:], in_=gate[:, :PAIR])
        for r in range(ROWS):
            load_expert_planes(w2sc, w2_scales, r)
        nc.sync.dma_start(out=g_rest[:], in_=gate[:, PAIR:])
        load_words(w2w[1], w2_words, *W2_LOADS[1])
        nc.sync.dma_start(out=v2w[:], in_=w2s_words[0].rearrange("p n d -> p (n d)").bitcast(I32))
        for r in range(ROWS):
            load_plane(v2sc, w2s_scales, r)

        def slots(a, b):
            return offsets[:, a * C // LIST_COLUMN : b * C // LIST_COLUMN]

        slot_words, slot_scales = {}, {}

        def gather_words(a, b):
            words = keep.tile([P, (b - a) * C], U32, name="xgw%d" % a, align_bytes=64)
            nc.vector.tensor_copy(out=words[:], in_=xw[:].indirect(slots(a, b)))
            for e in range(a, b):
                slot_words[e] = words[:, (e - a) * C : (e - a + 1) * C]

        def gather_scales(i):
            a, b = SCALE_GATHERS[i]
            scales = reuse.tile([P, (b - a) * C], U8, name="xgs%d" % a, align_bytes=64, offset=SCALES_AT[i])
            nc.vector.tensor_copy(out=scales[:], in_=xs[:].indirect(slots(a, b)))
            for e in range(a, b):
                slot_scales[e] = scales[:, (e - a) * C : (e - a + 1) * C]

        h_rows = {}

        def routed_activate(e):
            w = expert_words(w1w, W1_LOADS, e)
            pre = [bank[i] for i in ROUTED_PRE[e]]
            h_rows[e] = keep.tile([P, H], BF16, name="h_rows%d" % e, align_bytes=64)
            width = H // len(pre)
            for a in range(0, H, width):
                nc.tensor.matmul_mx(
                    out=pre[a // width][:, a : a + width],
                    lhsT=slot_words[e].bitcast(FP8X4), lhsT_scale=slot_scales[e],
                    rhs=w[:, 2 * a : 2 * (a + width)].bitcast(FP4X4), rhs_scale=w1sc[:, e, a : a + width],
                    start=True, stop=True,
                )
            for a in range(0, H, width):
                nc.scalar.activation(
                    out=h_rows[e][:].rearrange("s (u p v) -> s u p v", u=2, v=2)[:, :, a // PACK : (a + width) // PACK],
                    in_=pre[a // width][:, a : a + width].rearrange("s (p u v) -> s u p v", u=2, v=2), func=GELU,
                )

        def turned(pair):
            return bank[TURNED[pair]][:].rearrange("p (e u s) -> p e u s", e=2, u=2)

        def routed_turn(pair):
            for i in range(2):
                words = h_rows[2 * pair + i][:].bitcast(F32)
                for u in range(2):
                    nc.tensor.transpose(turned(pair)[:, i, u, :], words[:, u * P : (u + 1) * P], ident[:])

        h_in = [keep.tile([P, PAIR * PACK], BF16, name="h_in%d" % pair, align_bytes=64) for pair in range(PAIRS)]
        h_codes, gated = {}, {}

        def routed_interleave(pair, copy):
            copy(
                out=h_in[pair][:].bitcast(F32).rearrange("p (e s u) -> p e s u", e=2, u=2),
                in_=turned(pair).rearrange("p e u s -> p e s u"),
            )

        def routed_quantize(pair):
            if pair > 0:
                codes = reuse.tile([P, PAIR], U32, name="h_codes%d" % pair, align_bytes=64, offset=W2_FIRST_AT)
            else:
                codes = keep.tile([P, PAIR], U32, name="h_codes%d" % pair, align_bytes=64)
            scales = keep.tile([P, PAIR], U8, name="h_scales%d" % pair, align_bytes=64)
            nc.vector.quantize_mx(out=codes[:].bitcast(FP8X4), scales=scales[:], in_=h_in[pair][:])
            h_codes[pair] = (codes, scales)

        def routed_y(pair, nb):
            first = PAIR * nb if pair == 2 else 0
            return bank[ROUTED_Y[pair][nb]][:, first : first + PAIR]

        def routed_second(pair, nb):
            codes, scales = h_codes[pair]
            for i in range(2):
                e = 2 * pair + i
                cols = slice(i * C, (i + 1) * C)
                nc.tensor.matmul_mx(
                    out=bank[FIRST_Y[i]][:, cols] if (pair, nb) == (0, 0) else routed_y(pair, nb)[:, cols],
                    lhsT=expert_words(w2w, W2_LOADS, e)[:, 2 * nb * P : 2 * (nb + 1) * P].bitcast(FP4X4),
                    lhsT_scale=w2sc[:, e, nb * P : (nb + 1) * P],
                    rhs=codes[:, cols].bitcast(FP8X4), rhs_scale=scales[:, cols], start=True, stop=True,
                )

        def routed_gate(pair, nb):
            gated[pair, nb] = keep.tile([P, PAIR], F32, name="gated%d_%d" % (2 * pair, nb))
            nc.vector.tensor_tensor(out=gated[pair, nb][:], in0=routed_y(pair, nb), in1=g[pair], op=MULT)

        def scatter(pair, nb):
            places = win[nb][:].indirect(slots(2 * pair, 2 * pair + 2))
            if nb == 0:
                nc.vector.tensor_copy(out=places, in_=gated[pair, nb][:])
            else:
                nc.scalar.activation(out=places, in_=gated[pair, nb][:], func=COPY)

        def copy_out(pair, nb):
            gated[pair, nb] = keep.tile([P, PAIR], F32, name="plain%d_%d" % (2 * pair, nb))
            for i in range(2):
                cols = slice(i * C, (i + 1) * C)
                nc.scalar.copy(out=gated[pair, nb][:, cols], in_=bank[FIRST_Y[i]][:, cols])

        def scatter_gated(pair):
            places = win[0][:].indirect(slots(2 * pair, 2 * pair + 2))
            nc.vector.tensor_tensor(out=places, in0=gated[pair, 0][:], in1=g[pair], op=MULT)

        ys = {
            (c, nb): bank[SHARED_Y[c][nb][0]][:, SHARED_Y[c][nb][1] * CHUNK : (SHARED_Y[c][nb][1] + 1) * CHUNK]
            for c in range(CHUNKS) for nb in range(NB)
        }
        hs_in = [keep.tile([P, CHUNK * PACK], BF16, name="hs_in%d" % c, align_bytes=64) for c in range(CHUNKS)]

        def permute(src, dtype, run):
            dest = keep.tile([P, HS], dtype, name="perm%d" % run, align_bytes=64)
            nc.gpsimd.tensor_copy(
                out=dest[:].rearrange("p (d a b) -> p a d b", d=PACK, b=run),
                in_=src[:].rearrange("p (a b d) -> p a d b", d=PACK, b=run),
            )
            return dest

        def shared_activate(batch):
            pre = bank[SHARED_PRE[batch]][:].rearrange("p (d t) -> p d t", d=PACK)
            cols = slice(batch * P, (batch + 1) * P)
            for d in range(PACK):
                nc.tensor.matmul_mx(
                    out=pre[:, d, :], lhsT=v1w_perm[:, d * P : (d + 1) * P].bitcast(FP8X4),
                    lhsT_scale=v1sc_perm[:, d * P : (d + 1) * P],
                    rhs=xw[:, cols].bitcast(FP8X4), rhs_scale=xs[:, cols], start=True, stop=True,
                )
            c, place = divmod(batch * P, CHUNK)
            nc.scalar.activation(
                out=hs_in[c][:, place * PACK : (place + P) * PACK].rearrange("p (t d) -> p t d", d=PACK),
                in_=pre.rearrange("p d t -> p t d"), func=GELU,
            )

        hs_codes = {}

        def shared_quantize(c):
            codes = keep.tile([P, CHUNK], U32, name="hs_codes%d" % c, align_bytes=64)
            scales = keep.tile([P, CHUNK], U8, name="hs_scales%d" % c, align_bytes=64)
            nc.vector.quantize_mx(out=codes[:].bitcast(FP8X4), scales=scales[:], in_=hs_in[c][:])
            hs_codes[c] = (codes, scales)

        def shared_second(c, nb):
            codes, scales = hs_codes[c]
            nc.tensor.matmul_mx(
                out=ys[c, nb], lhsT=v2w[:, nb * P : (nb + 1) * P].bitcast(FP8X4),
                lhsT_scale=v2sc[:, nb * P : (nb + 1) * P],
                rhs=codes[:].bitcast(FP8X4), rhs_scale=scales[:], start=True, stop=True,
            )

        def finish(nb, c):
            cols = slice(c * CHUNK, (c + 1) * CHUNK)
            res = keep.tile([P, CHUNK], F32, name="res%d_%d" % (nb, c))
            nc.vector.tensor_tensor(out=res[:], in0=ys[c, nb], in1=win[nb][:, cols], op=ADD)
            nc.sync.dma_start(out=out[nb * P : (nb + 1) * P, cols], in_=res[:])

        gather_scales(0)
        gather_scales(1)
        for a, b in WORD_GATHERS:
            gather_words(a, b)
        v1sc_perm = permute(v1sc, U8, 16)
        v1w_perm = permute(v1w, I32, 4)
        for pair in range(2):
            routed_activate(2 * pair)
            routed_activate(2 * pair + 1)
            routed_turn(pair)
        gather_scales(2)
        routed_interleave(0, nc.vector.tensor_copy)

        routed_quantize(0)
        routed_second(0, 1)
        routed_second(0, 0)
        routed_activate(4)
        routed_activate(5)
        routed_interleave(1, nc.vector.tensor_copy)
        shared_activate(0)
        routed_gate(0, 1)
        copy_out(0, 0)
        routed_quantize(1)
        routed_second(1, 1)
        routed_second(1, 0)
        scatter_gated(0)
        scatter(0, 1)

        routed_turn(2)
        routed_interleave(2, nc.scalar.copy)
        shared_activate(1)
        routed_gate(1, 1)
        routed_gate(1, 0)
        routed_quantize(2)
        scatter(1, 0)

        shared_activate(2)
        shared_activate(3)
        scatter(1, 1)
        shared_activate(4)
        shared_activate(5)
        for c in range(2):
            shared_quantize(c)
            shared_second(c, 1)
        routed_second(2, 1)
        routed_second(2, 0)
        routed_gate(2, 0)
        routed_gate(2, 1)
        shared_second(0, 0)
        shared_second(1, 0)
        scatter(2, 0)
        scatter(2, 1)
        shared_quantize(2)
        shared_second(2, 0)
        shared_second(2, 1)

        for nb in range(NB):
            for c in range(CHUNKS):
                finish(nb, c)
